import numpy as np
import ml_dtypes


def mxq(x, axis, fmt="e4m3"):
    dtype, down = {"e4m3": (ml_dtypes.float8_e4m3fn, 7), "e5m2": (ml_dtypes.float8_e5m2, 14)}[fmt]
    v = np.moveaxis(np.asarray(x, np.float32).astype(ml_dtypes.bfloat16).astype(np.float64), axis, -1)
    blocks = v.reshape(v.shape[:-1] + (-1, 32))
    amax = np.abs(blocks).max(-1, keepdims=True)
    byte = np.maximum(np.where(amax > 0, np.frexp(amax)[1] - 1 + 127, 0) - down, 1)
    scale = np.exp2(byte - 127.0)
    codes = (blocks / scale).astype(np.float32).astype(dtype).astype(np.float64)
    return np.moveaxis((codes * scale).reshape(v.shape), -1, axis)


WIDE = False


def mx_kscale(k):
    if not WIDE:
        return np.ones(k)
    levels = np.array([10, -10, 5, -5, 0])
    if k % 512:
        return np.exp2(np.random.permutation(np.resize(levels, k // 32))).repeat(32)
    a = np.empty((k // 512, 16))
    for p in range(k // 512):
        a[p, :8] = np.random.permutation(np.resize(levels, 8))
        for g in range(8):
            far = levels[np.abs(levels - a[p, g]) >= 10]
            a[p, g + 8] = far[np.random.randint(len(far))]
    return np.exp2(a.ravel()).repeat(32)


def f64(x):
    return np.asarray(x).astype(np.float64)


def striped8(idx):
    return np.asarray(idx).reshape(8, -1, 16).transpose(0, 2, 1).reshape(128, -1).astype(np.uint16)


def unstriped8(offs):
    return offs.reshape(8, 16, -1).transpose(0, 2, 1).reshape(8, -1).astype(np.int64)


def pick8(x, idx, run):
    r = np.arange(len(x))
    return x[r[:, None], idx[r % (8 * run) // run]]


def sigmoid(v):
    return 1.0 / (1.0 + np.exp(-v))


D, T, I, Q, X, E = 512, 1024, 512, 256, 32, 512


def setup_inputs():
    n = np.random.standard_normal
    idx = np.stack([np.random.permutation(T)[:I] for _ in range(8)])
    fd = mx_kscale(D)
    fi = mx_kscale(I)
    ti = np.ones((8, T))
    np.put_along_axis(ti, idx, np.tile(fi, (8, 1)), axis=1)
    return {
        "query": (n((D, Q)) * (np.arange(D)[:, None] // 64 == np.arange(Q) % 8) * 0.0625 * fd[:, None]).astype(np.float32),
        "keys": (n((D, T)) / fd[:, None]).astype(np.float32),
        "kgate": (n((D, T))).astype(np.float32),
        "size": (np.random.uniform(0.5, 2.0, (1, I)) * fi).astype(np.float32),
        "vals": (n((E, T)) / ti[np.arange(E) % 512 // 64]).astype(np.float32),
        "own": ((np.arange(E)[:, None] // 64 == np.arange(Q) % 8) * 1.0).astype(np.float32),
        "offs": striped8(idx),
    }


def reference(query, keys, kgate, size, vals, own, offs):
    idx = unstriped8(offs)
    km = pick8(f64(keys), idx, 64) * sigmoid(pick8(f64(kgate), idx, 64))
    queryq = mxq(f64(query), 0, "e4m3")
    kmq = mxq(km, 0, "e4m3")
    a = queryq.T @ kmq
    p = np.exp(a - np.max(a, axis=1, keepdims=True))
    w = p * f64(size) / np.sum(p, axis=1, keepdims=True)
    wt = w.T
    vt = pick8(f64(vals), idx, 64).T
    vtq = mxq(vt, 0, "e4m3")
    wtq = mxq(wt, 0, "e4m3")
    o = vtq.T @ wtq
    ob = o * f64(own)
    y = ob.reshape(E, X, Q // X).sum(axis=2)
    return y

@@ -1,0 +1,201 @@
+from contextlib import ExitStack
+
+import concourse.mybir as mybir
+from concourse.masks import make_identity
+
+D, T, I, Q, X, E = 512, 1024, 512, 256, 32, 512
+FLOPS = 2 * D * Q * I + 2 * I * E * Q
+
+F32 = mybir.dt.float32
+BF16 = mybir.dt.bfloat16
+U32 = mybir.dt.uint32
+U16 = mybir.dt.uint16
+U8 = mybir.dt.uint8
+FP8X4 = mybir.dt.float8_e4m3fn_x4
+ACT = mybir.ActivationFunctionType
+ALU = mybir.AluOpType
+AXIS = mybir.AxisListType
+
+P = 128
+PACK = 4
+Q_TILES = Q // P
+HEADS = Q // X
+
+
+def quantize(nc, pool, grouped, width, name):
+    codes = pool.tile([P, width], U32, name=name + "_codes", align_bytes=64)
+    scales = pool.tile([P, width], U8, name=name + "_scales", align_bytes=64)
+    nc.vector.quantize_mx(out=codes[:].bitcast(FP8X4), scales=scales[:], in_=grouped)
+    return codes, scales
+
+
+def interleave(copy, grouped, planes):
+    copy(
+        out=grouped.rearrange("p (c i) t -> p c t i", i=4),
+        in_=planes.rearrange("p t (c i) -> p c t i", i=4),
+    )
+
+
+def tile_attend_ownlists_gatedkeys_kernel(tc, query, keys, kgate, size, vals, own, offs, out):
+    nc = tc.nc
+    with ExitStack() as ctx:
+        sb = ctx.enter_context(tc.tile_pool(name="sb", bufs=1))
+        ps = ctx.enter_context(tc.psum_pool(name="ps", bufs=1))
+
+        offsets = sb.tile([P, I // 16], U16, name="offsets")
+        nc.sync.dma_start(offsets[:], offs)
+
+        def plane_tiles(name):
+            return [sb.tile([P, T], F32, name=name + str(t), align_bytes=64) for t in range(PACK)]
+
+        def load_plane(tiles, src, t):
+            nc.sync.dma_start(out=tiles[t][:], in_=src.rearrange("(p t) n -> p t n", t=PACK)[:, t, :])
+
+        gate_pl, key_pl, val_pl = plane_tiles("gate"), plane_tiles("key"), plane_tiles("val")
+        load_plane(gate_pl, kgate, 0)
+        for t in range(PACK):
+            if t + 1 < PACK:
+                load_plane(gate_pl, kgate, t + 1)
+            load_plane(key_pl, keys, t)
+        q_raw = sb.tile([P, PACK, Q], F32, name="q_raw")
+        nc.sync.dma_start(out=q_raw[:], in_=query.rearrange("(p t) q -> p t q", t=PACK))
+        size_col = sb.tile([P, PACK], F32, name="size_col")
+        nc.sync.dma_start(out=size_col[:], in_=size.rearrange("o (p t) -> (o p) t", t=PACK))
+        for t in range(PACK):
+            load_plane(val_pl, vals, t)
+        own_sb = sb.tile([P, PACK, Q], F32, name="own_sb")
+        nc.sync.dma_start(out=own_sb[:], in_=own.rearrange("(p t) q -> p t q", t=PACK))
+
+        ident = sb.tile([P, P], F32, name="ident")
+        make_identity(nc, ident[:])
+
+        warm = sb.tile([P, 8], F32, name="warm")
+        nc.vector.memset(warm[:], 0.0)
+        warm_out = sb.tile([P, 8], F32, name="warm_out")
+        nc.scalar.activation(warm_out[:], warm[:], ACT.Sigmoid)
+
+        km = sb.tile([P, PACK, I], F32, name="km")
+        km_grouped = sb.tile([P, I, PACK], BF16, name="km_grouped", align_bytes=64)
+        gates = []
+        for t in range(PACK):
+            gate = sb.tile([P, I], F32, name="sig" + str(t))
+            nc.scalar.activation(gate[:], gate_pl[t][:].indirect(offsets[:]), ACT.Sigmoid)
+            nc.vector.tensor_tensor(km[:, t, :], key_pl[t][:].indirect(offsets[:]), gate[:], ALU.mult)
+            gates.append(gate)
+            if t % 2 == 1:
+                interleave(nc.vector.tensor_copy, km_grouped[:, :, t - 1 : t + 1], km[:, t - 1 : t + 1, :])
+        nc.scalar.activation(warm_out[:], gates[-1][:, 0:8], ACT.Exp)
+
+        km_codes, km_scales = quantize(nc, sb, km_grouped[:].rearrange("p c t -> p (c t)"), I, "km")
+
+        q_grouped = sb.tile([P, Q, PACK], BF16, name="q_grouped", align_bytes=64)
+        interleave(nc.scalar.copy, q_grouped[:], q_raw[:])
+        q_codes, q_scales = quantize(nc, sb, q_grouped[:].rearrange("p c t -> p (c t)"), Q, "q")
+
+        size_bc = ps.tile([P, PACK, P], F32, name="size_bc")
+        for t in range(PACK):
+            nc.tensor.transpose(size_bc[:, t, :], size_col[:, t : t + 1].to_broadcast([P, P]), ident[:])
+
+        scores = []
+        for qt in range(Q_TILES):
+            cols = slice(qt * P, (qt + 1) * P)
+            a = ps.tile([P, I], F32, name="score", tag="score", bufs=2)
+            nc.tensor.matmul_mx(
+                out=a[:], lhsT=q_codes[:, cols].bitcast(FP8X4), lhsT_scale=q_scales[:, cols],
+                rhs=km_codes[:].bitcast(FP8X4), rhs_scale=km_scales[:], start=True, stop=True,
+            )
+            scores.append(a)
+
+        def turn_words(turned, rows):
+            words = rows.bitcast(F32)
+            for u in range(2):
+                nc.tensor.transpose(turned[:, u, :], words[:, u : I // 2 : 2], ident[:])
+
+        v_turned = [ps.tile([P, 2, 2, P], F32, name="v_turned" + str(pair)) for pair in range(2)]
+
+        def round_values(t):
+            rounded = sb.tile([P, T], BF16, name="v_rounded" + str(t), align_bytes=64)
+            nc.scalar.activation(rounded[:], val_pl[t][:], ACT.Copy)
+            return rounded
+
+        def pick_on_scalar(t, rounded, tag):
+            picked = sb.tile([P, I], BF16, name="v_picked" + str(t), tag=tag, align_bytes=64)
+            nc.scalar.activation(picked[:], rounded[:].indirect(offsets[:]), ACT.Copy)
+            turn_words(v_turned[t // 2][:, t % 2], picked[:])
+
+        def pick_on_vector(t, tag):
+            picked = sb.tile([P, I], BF16, name="v_picked" + str(t), tag=tag, align_bytes=64)
+            nc.vector.tensor_copy(picked[:], val_pl[t][:].indirect(offsets[:]))
+            turn_words(v_turned[t // 2][:, t % 2], picked[:])
+
+        def group_values(pair, tag):
+            grouped = sb.tile([P, 2 * P * PACK], BF16, name="v_grouped" + str(pair), tag=tag, align_bytes=64)
+            nc.scalar.copy(
+                out=grouped[:].bitcast(F32).rearrange("p (k m u) -> p k m u", k=2, u=2),
+                in_=v_turned[pair][:].rearrange("p k u m -> p k m u"),
+            )
+            return quantize(nc, sb, grouped[:], 2 * P, "v" + str(pair))
+
+        pick_on_vector(1, "q_grouped")
+        pick_on_scalar(0, round_values(0), "v_picked0")
+        rounded2 = round_values(2)
+
+        totals = sb.tile([P, Q_TILES], F32, name="totals")
+        probs = []
+        both = sb.tile([P, Q_TILES, I], F32, name="p", tag="val2", align_bytes=64)
+        neg_max = sb.tile([P, Q_TILES], F32, name="neg_max", tag="val1", align_bytes=64)
+        for qt in range(Q_TILES):
+            negated = sb.tile([P, I], F32, name="negated", tag="negated" + str(qt), align_bytes=64)
+            nc.vector.tensor_scalar(
+                negated[:], scores[qt][:], -1.0, None, ALU.mult, ALU.min, accum_out=neg_max[:, qt : qt + 1]
+            )
+            p = both[:, qt, :]
+            nc.scalar.activation(
+                p, scores[qt][:], ACT.Exp, bias=neg_max[:, qt : qt + 1], accum_out=totals[:, qt : qt + 1]
+            )
+            probs.append(p)
+
+        pick_on_vector(3, "negated1")
+        inv = sb.tile([P, Q_TILES], F32, name="inv", tag="val3", align_bytes=64)
+        nc.vector.reciprocal(inv[:], totals[:])
+        w_turned = []
+        for qt in range(Q_TILES):
+            w = sb.tile([P, I], BF16, name="w" + str(qt), align_bytes=64)
+            nc.vector.scalar_tensor_tensor(
+                w[:].rearrange("p (s t) -> p s t", t=PACK), probs[qt].rearrange("p (s t) -> p s t", t=PACK),
+                inv[:, qt : qt + 1], size_bc[:].rearrange("p t s -> p s t"), ALU.mult, ALU.mult,
+            )
+            turned = ps.tile([P, 2, P], F32, name="w_turned", tag="score", bufs=2)
+            turn_words(turned[:], w[:])
+            w_turned.append(turned)
+        pick_on_scalar(2, rounded2, "val1")
+
+        v_mx = [group_values(0, "v_rounded2"), group_values(1, "v_grouped1")]
+
+        w_mx = []
+        result = sb.tile([P, PACK, X], F32, name="result")
+        for qt in range(Q_TILES):
+            w_grouped = sb.tile([P, P * PACK], BF16, name="w_grouped" + str(qt), align_bytes=64)
+            nc.scalar.copy(
+                out=w_grouped[:].bitcast(F32).rearrange("p (q u) -> p q u", u=2),
+                in_=w_turned[qt][:].rearrange("p u q -> p q u"),
+            )
+            w_codes, w_scales = quantize(nc, sb, w_grouped[:], P, "w" + str(qt))
+            o = ps.tile([P, PACK, P], F32, name="o" + str(qt))
+            for t in range(PACK):
+                v_codes, v_scales = v_mx[t // 2]
+                cols = slice((t % 2) * P, (t % 2 + 1) * P)
+                nc.tensor.matmul_mx(
+                    out=o[:, t, :], lhsT=v_codes[:, cols].bitcast(FP8X4), lhsT_scale=v_scales[:, cols],
+                    rhs=w_codes[:].bitcast(FP8X4), rhs_scale=w_scales[:], start=True, stop=True,
+                )
+            w_mx.append(o)
+        for qt in range(Q_TILES):
+            owned = sb.tile([P, PACK, P], F32, name="owned" + str(qt))
+            nc.vector.tensor_tensor(owned[:], w_mx[qt][:], own_sb[:, :, qt * P : (qt + 1) * P], ALU.mult)
+            places = P // HEADS
+            nc.vector.tensor_reduce(
+                result[:, :, qt * places : (qt + 1) * places],
+                owned[:].rearrange("p t (x j) -> p t x j", j=HEADS), AXIS.X, ALU.add,
+            )
+        nc.sync.dma_start(out=out.rearrange("(p t) x -> p t x", t=PACK), in_=result[:])

@@ -22,8 +22,8 @@ Q_TILES = Q // P
 HEADS = Q // X
 
 
-def quantize(nc, pool, grouped, width, name):
-    codes = pool.tile([P, width], U32, name=name + "_codes", align_bytes=64)
+def quantize(nc, pool, grouped, width, name, tag=""):
+    codes = pool.tile([P, width], U32, name=name + "_codes", tag=tag or name + "_codes", align_bytes=64)
     scales = pool.tile([P, width], U8, name=name + "_scales", align_bytes=64)
     nc.vector.quantize_mx(out=codes[:].bitcast(FP8X4), scales=scales[:], in_=grouped)
     return codes, scales
@@ -43,7 +43,6 @@ def tile_attend_ownlists_gatedkeys_kernel(tc, query, keys, kgate, size, vals, ow
         ps = ctx.enter_context(tc.psum_pool(name="ps", bufs=1))
 
         offsets = sb.tile([P, I // 16], U16, name="offsets")
-        nc.sync.dma_start(offsets[:], offs)
 
         def plane_tiles(name):
             return [sb.tile([P, T], F32, name=name + str(t), align_bytes=64) for t in range(PACK)]
@@ -53,6 +52,7 @@ def tile_attend_ownlists_gatedkeys_kernel(tc, query, keys, kgate, size, vals, ow
 
         gate_pl, key_pl, val_pl = plane_tiles("gate"), plane_tiles("key"), plane_tiles("val")
         load_plane(gate_pl, kgate, 0)
+        nc.sync.dma_start(offsets[:], offs)
         for t in range(PACK):
             if t + 1 < PACK:
                 load_plane(gate_pl, kgate, t + 1)
@@ -60,9 +60,13 @@ def tile_attend_ownlists_gatedkeys_kernel(tc, query, keys, kgate, size, vals, ow
         q_raw = sb.tile([P, PACK, Q], F32, name="q_raw")
         nc.sync.dma_start(out=q_raw[:], in_=query.rearrange("(p t) q -> p t q", t=PACK))
         size_col = sb.tile([P, PACK], F32, name="size_col")
-        nc.sync.dma_start(out=size_col[:], in_=size.rearrange("o (p t) -> (o p) t", t=PACK))
         for t in range(PACK):
             load_plane(val_pl, vals, t)
+            if t < 2:
+                nc.sync.dma_start(
+                    out=size_col[t * 64 : (t + 1) * 64, :].rearrange("p (s e) -> p s e", e=2),
+                    in_=size.rearrange("o (p s u e) -> (o p) s u e", s=2, u=2, e=2)[:, :, t, :],
+                )
         own_sb = sb.tile([P, PACK, Q], F32, name="own_sb")
         nc.sync.dma_start(out=own_sb[:], in_=own.rearrange("(p t) q -> p t q", t=PACK))
 
@@ -83,14 +87,17 @@ def tile_attend_ownlists_gatedkeys_kernel(tc, query, keys, kgate, size, vals, ow
             nc.vector.tensor_tensor(km[:, t, :], key_pl[t][:].indirect(offsets[:]), gate[:], ALU.mult)
             gates.append(gate)
             if t % 2 == 1:
-                interleave(nc.vector.tensor_copy, km_grouped[:, :, t - 1 : t + 1], km[:, t - 1 : t + 1, :])
+                nc.vector.tensor_copy(
+                    out=km_grouped[:, :, t - 1 : t + 1].rearrange("p (u s e) t -> p s t u e", u=2, e=2),
+                    in_=km[:, t - 1 : t + 1, :].rearrange("p t (s u e) -> p s t u e", u=2, e=2),
+                )
         nc.scalar.activation(warm_out[:], gates[-1][:, 0:8], ACT.Exp)
 
-        km_codes, km_scales = quantize(nc, sb, km_grouped[:].rearrange("p c t -> p (c t)"), I, "km")
 
         q_grouped = sb.tile([P, Q, PACK], BF16, name="q_grouped", align_bytes=64)
         interleave(nc.scalar.copy, q_grouped[:], q_raw[:])
         q_codes, q_scales = quantize(nc, sb, q_grouped[:].rearrange("p c t -> p (c t)"), Q, "q")
+        km_codes, km_scales = quantize(nc, sb, km_grouped[:].rearrange("p c t -> p (c t)"), I, "km", "q_grouped")
 
         size_bc = ps.tile([P, PACK, P], F32, name="size_bc")
         for t in range(PACK):
@@ -136,7 +143,7 @@ def tile_attend_ownlists_gatedkeys_kernel(tc, query, keys, kgate, size, vals, ow
             )
             return quantize(nc, sb, grouped[:], 2 * P, "v" + str(pair))
 
-        pick_on_vector(1, "q_grouped")
+        pick_on_vector(1, "km_grouped")
         pick_on_scalar(0, round_values(0), "v_picked0")
         rounded2 = round_values(2)
 
@@ -145,10 +152,13 @@ def tile_attend_ownlists_gatedkeys_kernel(tc, query, keys, kgate, size, vals, ow
         both = sb.tile([P, Q_TILES, I], F32, name="p", tag="val2", align_bytes=64)
         neg_max = sb.tile([P, Q_TILES], F32, name="neg_max", tag="val1", align_bytes=64)
         for qt in range(Q_TILES):
-            negated = sb.tile([P, I], F32, name="negated", tag="negated" + str(qt), align_bytes=64)
-            nc.vector.tensor_scalar(
-                negated[:], scores[qt][:], -1.0, None, ALU.mult, ALU.min, accum_out=neg_max[:, qt : qt + 1]
-            )
+            if qt == 0:
+                nc.vector.tensor_reduce(neg_max[:, 0:1], scores[qt][:], AXIS.X, ALU.max, negate=True)
+            else:
+                negated = sb.tile([P, I], F32, name="negated1", align_bytes=64)
+                nc.vector.tensor_scalar(
+                    negated[:], scores[qt][:], -1.0, None, ALU.mult, ALU.min, accum_out=neg_max[:, qt : qt + 1]
+                )
             p = both[:, qt, :]
             nc.scalar.activation(
                 p, scores[qt][:], ACT.Exp, bias=neg_max[:, qt : qt + 1], accum_out=totals[:, qt : qt + 1]
@@ -156,27 +166,30 @@ def tile_attend_ownlists_gatedkeys_kernel(tc, query, keys, kgate, size, vals, ow
             probs.append(p)
 
         pick_on_vector(3, "negated1")
-        inv = sb.tile([P, Q_TILES], F32, name="inv", tag="val3", align_bytes=64)
-        nc.vector.reciprocal(inv[:], totals[:])
+        inv = sb.tile([P, Q_TILES], F32, name="inv")
+        minus_one = sb.tile([P, Q_TILES], F32, name="minus_one")
+        nc.gpsimd.memset(minus_one[:], -1.0)
+        nc.gpsimd.tensor_tensor(inv[:], totals[:], minus_one[:], ALU.pow)
+        w_both = sb.tile([P, Q_TILES, I], BF16, name="w", tag="val3", align_bytes=64)
         w_turned = []
         for qt in range(Q_TILES):
-            w = sb.tile([P, I], BF16, name="w" + str(qt), align_bytes=64)
+            w = w_both[:, qt, :]
             nc.vector.scalar_tensor_tensor(
-                w[:].rearrange("p (s t) -> p s t", t=PACK), probs[qt].rearrange("p (s t) -> p s t", t=PACK),
+                w.rearrange("p (s t) -> p s t", t=PACK), probs[qt].rearrange("p (s t) -> p s t", t=PACK),
                 inv[:, qt : qt + 1], size_bc[:].rearrange("p t s -> p s t"), ALU.mult, ALU.mult,
             )
             turned = ps.tile([P, 2, P], F32, name="w_turned", tag="score", bufs=2)
-            turn_words(turned[:], w[:])
+            for u in range(2):
+                nc.tensor.transpose(turned[:, u, :], w.bitcast(F32)[:, u * P : (u + 1) * P], ident[:])
             w_turned.append(turned)
         pick_on_scalar(2, rounded2, "val1")
 
         v_mx = [group_values(0, "v_rounded2"), group_values(1, "v_grouped1")]
 
         w_mx = []
-        result = sb.tile([P, PACK, X], F32, name="result")
         for qt in range(Q_TILES):
             w_grouped = sb.tile([P, P * PACK], BF16, name="w_grouped" + str(qt), align_bytes=64)
-            nc.scalar.copy(
+            (nc.vector.tensor_copy, nc.scalar.copy)[qt](
                 out=w_grouped[:].bitcast(F32).rearrange("p (q u) -> p q u", u=2),
                 in_=w_turned[qt][:].rearrange("p u q -> p q u"),
             )
@@ -190,12 +203,13 @@ def tile_attend_ownlists_gatedkeys_kernel(tc, query, keys, kgate, size, vals, ow
                     rhs=w_codes[:].bitcast(FP8X4), rhs_scale=w_scales[:], start=True, stop=True,
                 )
             w_mx.append(o)
+        places = P // HEADS
+        owned = []
         for qt in range(Q_TILES):
-            owned = sb.tile([P, PACK, P], F32, name="owned" + str(qt))
-            nc.vector.tensor_tensor(owned[:], w_mx[qt][:], own_sb[:, :, qt * P : (qt + 1) * P], ALU.mult)
-            places = P // HEADS
-            nc.vector.tensor_reduce(
-                result[:, :, qt * places : (qt + 1) * places],
-                owned[:].rearrange("p t (x j) -> p t x j", j=HEADS), AXIS.X, ALU.add,
-            )
+            ob = sb.tile([P, PACK, P], F32, name="owned" + str(qt))
+            nc.vector.tensor_tensor(ob[:], w_mx[qt][:], own_sb[:, :, qt * P : (qt + 1) * P], ALU.mult)
+            owned.append(ob[:].rearrange("p t (x j) -> p t x j", j=HEADS))
+        result = sb.tile([P, PACK, X], F32, name="result", tag="w1_codes", align_bytes=64)
+        for qt in range(Q_TILES):
+            nc.vector.tensor_reduce(result[:, :, qt * places : (qt + 1) * places], owned[qt], AXIS.X, ALU.add)
         nc.sync.dma_start(out=out.rearrange("(p t) x -> p t x", t=PACK), in_=result[:])

@@ -20,20 +20,7 @@ P = 128
 PACK = 4
 Q_TILES = Q // P
 HEADS = Q // X
-
-
-def quantize(nc, pool, grouped, width, name, tag=""):
-    codes = pool.tile([P, width], U32, name=name + "_codes", tag=tag or name + "_codes", align_bytes=64)
-    scales = pool.tile([P, width], U8, name=name + "_scales", align_bytes=64)
-    nc.vector.quantize_mx(out=codes[:].bitcast(FP8X4), scales=scales[:], in_=grouped)
-    return codes, scales
-
-
-def interleave(copy, grouped, planes):
-    copy(
-        out=grouped.rearrange("p (c i) t -> p c t i", i=4),
-        in_=planes.rearrange("p t (c i) -> p c t i", i=4),
-    )
+HALF = I // 2
 
 
 def tile_attend_ownlists_gatedkeys_kernel(tc, query, keys, kgate, size, vals, own, offs, out):
@@ -42,7 +29,27 @@ def tile_attend_ownlists_gatedkeys_kernel(tc, query, keys, kgate, size, vals, ow
         sb = ctx.enter_context(tc.tile_pool(name="sb", bufs=1))
         ps = ctx.enter_context(tc.psum_pool(name="ps", bufs=1))
 
+        def mx_tiles(width, name, tag=""):
+            codes = sb.tile([P, width], U32, name=name + "_codes", tag=tag or name + "_codes", align_bytes=64)
+            scales = sb.tile([P, width], U8, name=name + "_scales", align_bytes=64)
+            return codes, scales
+
+        def quantize(mx, cols, grouped):
+            nc.vector.quantize_mx(out=mx[0][:, cols].bitcast(FP8X4), scales=mx[1][:, cols], in_=grouped)
+
+        def product(dst, lhs, lhs_cols, rhs, rhs_cols):
+            nc.tensor.matmul_mx(
+                out=dst, lhsT=lhs[0][:, lhs_cols].bitcast(FP8X4), lhsT_scale=lhs[1][:, lhs_cols],
+                rhs=rhs[0][:, rhs_cols].bitcast(FP8X4), rhs_scale=rhs[1][:, rhs_cols], start=True, stop=True,
+            )
+
+        def word(tile, col):
+            return tile[:, col : col + 2].bitcast(F32)
+
         offsets = sb.tile([P, I // 16], U16, name="offsets")
+
+        def listed(plane, slots):
+            return plane[:].indirect(offsets[:, slots.start // 16 : slots.stop // 16])
 
         def plane_tiles(name):
             return [sb.tile([P, T], F32, name=name + str(t), align_bytes=64) for t in range(PACK)]
@@ -50,23 +57,24 @@ def tile_attend_ownlists_gatedkeys_kernel(tc, query, keys, kgate, size, vals, ow
         def load_plane(tiles, src, t):
             nc.sync.dma_start(out=tiles[t][:], in_=src.rearrange("(p t) n -> p t n", t=PACK)[:, t, :])
 
+        every, lower, upper = slice(0, I), slice(0, HALF), slice(HALF, I)
+        q_cols = [slice(qt * P, (qt + 1) * P) for qt in range(Q_TILES)]
+
         gate_pl, key_pl, val_pl = plane_tiles("gate"), plane_tiles("key"), plane_tiles("val")
+        size_col = sb.tile([P, PACK], F32, name="size_col")
+        nc.scalar.dma_start(out=size_col[:], in_=size.rearrange("o (p t) -> (o p) t", t=PACK))
         load_plane(gate_pl, kgate, 0)
         nc.sync.dma_start(offsets[:], offs)
-        for t in range(PACK):
-            if t + 1 < PACK:
-                load_plane(gate_pl, kgate, t + 1)
-            load_plane(key_pl, keys, t)
-        q_raw = sb.tile([P, PACK, Q], F32, name="q_raw")
+        load_plane(key_pl, keys, 0)
+        load_plane(gate_pl, kgate, 1)
+        load_plane(key_pl, keys, 1)
+        for tiles, src in ((gate_pl, kgate), (key_pl, keys)):
+            for t in (2, 3):
+                load_plane(tiles, src, t)
+        q_raw = sb.tile([P, PACK, Q], F32, name="q_raw", align_bytes=64)
         nc.sync.dma_start(out=q_raw[:], in_=query.rearrange("(p t) q -> p t q", t=PACK))
-        size_col = sb.tile([P, PACK], F32, name="size_col")
         for t in range(PACK):
             load_plane(val_pl, vals, t)
-            if t < 2:
-                nc.sync.dma_start(
-                    out=size_col[t * 64 : (t + 1) * 64, :].rearrange("p (s e) -> p s e", e=2),
-                    in_=size.rearrange("o (p s u e) -> (o p) s u e", s=2, u=2, e=2)[:, :, t, :],
-                )
         own_sb = sb.tile([P, PACK, Q], F32, name="own_sb")
         nc.sync.dma_start(out=own_sb[:], in_=own.rearrange("(p t) q -> p t q", t=PACK))
 
@@ -78,138 +86,133 @@ def tile_attend_ownlists_gatedkeys_kernel(tc, query, keys, kgate, size, vals, ow
         warm_out = sb.tile([P, 8], F32, name="warm_out")
         nc.scalar.activation(warm_out[:], warm[:], ACT.Sigmoid)
 
-        km = sb.tile([P, PACK, I], F32, name="km")
-        km_grouped = sb.tile([P, I, PACK], BF16, name="km_grouped", align_bytes=64)
-        gates = []
+        size_turned = ps.tile([P, PACK, P], F32, name="size_turned", tag="out0")
         for t in range(PACK):
-            gate = sb.tile([P, I], F32, name="sig" + str(t))
-            nc.scalar.activation(gate[:], gate_pl[t][:].indirect(offsets[:]), ACT.Sigmoid)
-            nc.vector.tensor_tensor(km[:, t, :], key_pl[t][:].indirect(offsets[:]), gate[:], ALU.mult)
-            gates.append(gate)
-            if t % 2 == 1:
-                nc.vector.tensor_copy(
-                    out=km_grouped[:, :, t - 1 : t + 1].rearrange("p (u s e) t -> p s t u e", u=2, e=2),
-                    in_=km[:, t - 1 : t + 1, :].rearrange("p t (s u e) -> p s t u e", u=2, e=2),
-                )
-        nc.scalar.activation(warm_out[:], gates[-1][:, 0:8], ACT.Exp)
+            nc.tensor.transpose(size_turned[:, t, :], size_col[:, t : t + 1].to_broadcast([P, P]), ident[:])
+        size_all = sb.tile([P, I], F32, name="size_all", align_bytes=64)
+        nc.vector.tensor_copy(
+            out=size_all[:].rearrange("p (u s e) -> p u s e", u=2, e=2),
+            in_=size_turned[:].rearrange("p (u e) s -> p u s e", u=2),
+        )
 
+        km = [sb.tile([P, 2, I], F32, name="km" + str(pair)) for pair in range(2)]
+        km_grouped = sb.tile([P, I * PACK + HALF], BF16, name="km_grouped", align_bytes=64)
+        km_view = km_grouped[:, 0 : I * PACK].rearrange("p (c i t) -> p c t i", i=4, t=PACK)
+        gates = [sb.tile([P, I], F32, name="sig" + str(t)) for t in range(PACK)]
 
-        q_grouped = sb.tile([P, Q, PACK], BF16, name="q_grouped", align_bytes=64)
-        interleave(nc.scalar.copy, q_grouped[:], q_raw[:])
-        q_codes, q_scales = quantize(nc, sb, q_grouped[:].rearrange("p c t -> p (c t)"), Q, "q")
-        km_codes, km_scales = quantize(nc, sb, km_grouped[:].rearrange("p c t -> p (c t)"), I, "km", "q_grouped")
-
-        size_bc = ps.tile([P, PACK, P], F32, name="size_bc")
-        for t in range(PACK):
-            nc.tensor.transpose(size_bc[:, t, :], size_col[:, t : t + 1].to_broadcast([P, P]), ident[:])
-
-        scores = []
-        for qt in range(Q_TILES):
-            cols = slice(qt * P, (qt + 1) * P)
-            a = ps.tile([P, I], F32, name="score", tag="score", bufs=2)
-            nc.tensor.matmul_mx(
-                out=a[:], lhsT=q_codes[:, cols].bitcast(FP8X4), lhsT_scale=q_scales[:, cols],
-                rhs=km_codes[:].bitcast(FP8X4), rhs_scale=km_scales[:], start=True, stop=True,
+        def weave_keys(pair, slots):
+            nc.vector.tensor_copy(
+                out=km_view[:, slots.start // 4 : slots.stop // 4, 2 * pair : 2 * pair + 2, :],
+                in_=km[pair][:, :, slots].rearrange("p t (c i) -> p c t i", i=4),
             )
-            scores.append(a)
 
-        def turn_words(turned, rows):
-            words = rows.bitcast(F32)
-            for u in range(2):
-                nc.tensor.transpose(turned[:, u, :], words[:, u : I // 2 : 2], ident[:])
+        for t in range(PACK):
+            nc.scalar.activation(gates[t][:], listed(gate_pl[t], every), ACT.Sigmoid)
+            for slots in (every,) if t < PACK - 1 else (lower, upper):
+                nc.vector.tensor_tensor(
+                    km[t // 2][:, t % 2, slots], listed(key_pl[t], slots), gates[t][:, slots], ALU.mult
+                )
+            if t == 1:
+                weave_keys(0, every)
+        nc.scalar.activation(warm_out[:], gates[-1][:, 0:8], ACT.Exp)
+        weave_keys(1, lower)
+        weave_keys(1, upper)
+
+        q_grouped = sb.tile([P, Q * PACK], BF16, name="q_grouped", align_bytes=64)
+        v_grouped = sb.tile([P, PACK * I], BF16, name="v_grouped", tag="val0", align_bytes=64)
+        w_rows = [sb.tile([P, I], BF16, name="w_rows" + str(qt), align_bytes=64)[:] for qt in range(Q_TILES)]
+        picked = [sb.tile([P, I], BF16, name="picked" + str(t), align_bytes=64)[:] for t in (1, 2, 3)]
+        picked.insert(0, km_grouped[:, I * PACK - HALF : I * PACK + HALF])
+        neg_max = [word(v_grouped, 2 * qt) for qt in range(Q_TILES)]
+        totals = sb.tile([P, Q_TILES], F32, name="totals")
+
+        def pick(on_scalar, t, slots):
+            if on_scalar:
+                nc.scalar.activation(picked[t][:, slots], listed(val_pl[t], slots), ACT.Copy)
+            else:
+                nc.vector.tensor_copy(picked[t][:, slots], listed(val_pl[t], slots))
 
         v_turned = [ps.tile([P, 2, 2, P], F32, name="v_turned" + str(pair)) for pair in range(2)]
 
-        def round_values(t):
-            rounded = sb.tile([P, T], BF16, name="v_rounded" + str(t), align_bytes=64)
-            nc.scalar.activation(rounded[:], val_pl[t][:], ACT.Copy)
-            return rounded
+        def turn_values(t):
+            words = picked[t].bitcast(F32)
+            for u in range(2):
+                nc.tensor.transpose(v_turned[t // 2][:, t % 2, u, :], words[:, u : I // 2 : 2], ident[:])
 
-        def pick_on_scalar(t, rounded, tag):
-            picked = sb.tile([P, I], BF16, name="v_picked" + str(t), tag=tag, align_bytes=64)
-            nc.scalar.activation(picked[:], rounded[:].indirect(offsets[:]), ACT.Copy)
-            turn_words(v_turned[t // 2][:, t % 2], picked[:])
-
-        def pick_on_vector(t, tag):
-            picked = sb.tile([P, I], BF16, name="v_picked" + str(t), tag=tag, align_bytes=64)
-            nc.vector.tensor_copy(picked[:], val_pl[t][:].indirect(offsets[:]))
-            turn_words(v_turned[t // 2][:, t % 2], picked[:])
-
-        def group_values(pair, tag):
-            grouped = sb.tile([P, 2 * P * PACK], BF16, name="v_grouped" + str(pair), tag=tag, align_bytes=64)
-            nc.scalar.copy(
-                out=grouped[:].bitcast(F32).rearrange("p (k m u) -> p k m u", k=2, u=2),
-                in_=v_turned[pair][:].rearrange("p k u m -> p k m u"),
+        def group(copy, turned, grouped):
+            copy(
+                out=grouped.bitcast(F32).rearrange("p (k m u) -> p k m u", m=P, u=2),
+                in_=turned[:].rearrange("p k u m -> p k m u"),
             )
-            return quantize(nc, sb, grouped[:], 2 * P, "v" + str(pair))
 
-        pick_on_vector(1, "km_grouped")
-        pick_on_scalar(0, round_values(0), "v_picked0")
-        rounded2 = round_values(2)
+        nc.scalar.copy(
+            out=q_grouped[:].rearrange("p (c i t) -> p c t i", i=4, t=PACK),
+            in_=q_raw[:].rearrange("p t (c i) -> p c t i", i=4),
+        )
+        km_mx = [mx_tiles(HALF, "km0"), mx_tiles(HALF, "km1", "q_grouped")]
+        q_mx = mx_tiles(Q, "q")
+        quantize(km_mx[0], lower, km_grouped[:, 0 : HALF * PACK])
+        quantize(q_mx, slice(0, Q), q_grouped[:])
+        quantize(km_mx[1], lower, km_grouped[:, HALF * PACK : I * PACK])
 
-        totals = sb.tile([P, Q_TILES], F32, name="totals")
-        probs = []
-        both = sb.tile([P, Q_TILES, I], F32, name="p", tag="val2", align_bytes=64)
-        neg_max = sb.tile([P, Q_TILES], F32, name="neg_max", tag="val1", align_bytes=64)
+        scores = [ps.tile([P, I], F32, name="score", tag="score" + str(qt)) for qt in range(Q_TILES)]
+        for h, slots in enumerate((lower, upper)):
+            for qt in range(Q_TILES):
+                product(scores[qt][:, slots], q_mx, q_cols[qt], km_mx[h], lower)
+
+        pick(True, 0, upper)
+        pick(False, 0, lower)
+        pick(True, 1, every)
+        pick(True, 2, every)
+        for t in range(3):
+            turn_values(t)
+
+        probs = sb.tile([P, Q_TILES * I], F32, name="probs", tag="val2", align_bytes=64)
+        inv0 = sb.tile([P, Q_TILES], F32, name="inv0", tag="val3", align_bytes=64)
+        inv = [inv0[:, qt : qt + 1] for qt in range(Q_TILES)]
         for qt in range(Q_TILES):
-            if qt == 0:
-                nc.vector.tensor_reduce(neg_max[:, 0:1], scores[qt][:], AXIS.X, ALU.max, negate=True)
-            else:
-                negated = sb.tile([P, I], F32, name="negated1", align_bytes=64)
-                nc.vector.tensor_scalar(
-                    negated[:], scores[qt][:], -1.0, None, ALU.mult, ALU.min, accum_out=neg_max[:, qt : qt + 1]
-                )
-            p = both[:, qt, :]
+            nc.vector.tensor_reduce(neg_max[qt], scores[qt][:], AXIS.X, ALU.max, negate=True)
             nc.scalar.activation(
-                p, scores[qt][:], ACT.Exp, bias=neg_max[:, qt : qt + 1], accum_out=totals[:, qt : qt + 1]
+                probs[:, qt * I : (qt + 1) * I].rearrange("p (u s e) -> p u s e", u=2, e=2),
+                scores[qt][:].rearrange("p (s u e) -> p u s e", u=2, e=2),
+                ACT.Exp, bias=neg_max[qt], accum_out=totals[:, qt : qt + 1],
             )
-            probs.append(p)
+        pick(False, 3, every)
+        for qt in range(Q_TILES):
+            nc.vector.reciprocal(inv[qt], totals[:, qt : qt + 1])
+        turn_values(3)
+        for pair in range(2):
+            group(nc.scalar.copy, v_turned[pair], v_grouped[:, pair * 2 * I : (pair + 1) * 2 * I])
 
-        pick_on_vector(3, "negated1")
-        inv = sb.tile([P, Q_TILES], F32, name="inv")
-        minus_one = sb.tile([P, Q_TILES], F32, name="minus_one")
-        nc.gpsimd.memset(minus_one[:], -1.0)
-        nc.gpsimd.tensor_tensor(inv[:], totals[:], minus_one[:], ALU.pow)
-        w_both = sb.tile([P, Q_TILES, I], BF16, name="w", tag="val3", align_bytes=64)
         w_turned = []
         for qt in range(Q_TILES):
-            w = w_both[:, qt, :]
             nc.vector.scalar_tensor_tensor(
-                w.rearrange("p (s t) -> p s t", t=PACK), probs[qt].rearrange("p (s t) -> p s t", t=PACK),
-                inv[:, qt : qt + 1], size_bc[:].rearrange("p t s -> p s t"), ALU.mult, ALU.mult,
+                w_rows[qt], probs[:, qt * I : (qt + 1) * I], inv[qt], size_all[:], ALU.mult, ALU.mult
             )
-            turned = ps.tile([P, 2, P], F32, name="w_turned", tag="score", bufs=2)
+            turned = ps.tile([P, 1, 2, P], F32, name="w_turned", tag="score" + str(qt))
             for u in range(2):
-                nc.tensor.transpose(turned[:, u, :], w.bitcast(F32)[:, u * P : (u + 1) * P], ident[:])
+                nc.tensor.transpose(turned[:, 0, u, :], w_rows[qt].bitcast(F32)[:, u * P : (u + 1) * P], ident[:])
             w_turned.append(turned)
-        pick_on_scalar(2, rounded2, "val1")
 
-        v_mx = [group_values(0, "v_rounded2"), group_values(1, "v_grouped1")]
-
-        w_mx = []
+        w_grouped = sb.tile([P, Q * PACK], BF16, name="w_grouped", align_bytes=64)
+        v_mx = mx_tiles(PACK * P, "v", "val2")
+        quantize(v_mx, slice(0, 2 * P), v_grouped[:, 0 : 2 * I])
+        w_mx = [mx_tiles(P, "w" + str(qt)) for qt in range(Q_TILES)]
         for qt in range(Q_TILES):
-            w_grouped = sb.tile([P, P * PACK], BF16, name="w_grouped" + str(qt), align_bytes=64)
-            (nc.vector.tensor_copy, nc.scalar.copy)[qt](
-                out=w_grouped[:].bitcast(F32).rearrange("p (q u) -> p q u", u=2),
-                in_=w_turned[qt][:].rearrange("p u q -> p q u"),
-            )
-            w_codes, w_scales = quantize(nc, sb, w_grouped[:], P, "w" + str(qt))
-            o = ps.tile([P, PACK, P], F32, name="o" + str(qt))
+            group(nc.scalar.copy, w_turned[qt], w_grouped[:, qt * I : (qt + 1) * I])
+            quantize(w_mx[qt], slice(0, P), w_grouped[:, qt * I : (qt + 1) * I])
+            if qt == 0:
+                quantize(v_mx, slice(2 * P, 4 * P), v_grouped[:, 2 * I : 4 * I])
+
+        result = sb.tile([P, PACK, X], F32, name="result", align_bytes=64)
+        owned = sb.tile([P, PACK, Q], F32, name="owned", tag="w_grouped", align_bytes=64)
+        for qt in range(Q_TILES):
+            o = ps.tile([P, PACK, P], F32, name="o", tag="out" + str(qt))
             for t in range(PACK):
-                v_codes, v_scales = v_mx[t // 2]
-                cols = slice((t % 2) * P, (t % 2 + 1) * P)
-                nc.tensor.matmul_mx(
-                    out=o[:, t, :], lhsT=v_codes[:, cols].bitcast(FP8X4), lhsT_scale=v_scales[:, cols],
-                    rhs=w_codes[:].bitcast(FP8X4), rhs_scale=w_scales[:], start=True, stop=True,
-                )
-            w_mx.append(o)
-        places = P // HEADS
-        owned = []
-        for qt in range(Q_TILES):
-            ob = sb.tile([P, PACK, P], F32, name="owned" + str(qt))
-            nc.vector.tensor_tensor(ob[:], w_mx[qt][:], own_sb[:, :, qt * P : (qt + 1) * P], ALU.mult)
-            owned.append(ob[:].rearrange("p t (x j) -> p t x j", j=HEADS))
-        result = sb.tile([P, PACK, X], F32, name="result", tag="w1_codes", align_bytes=64)
-        for qt in range(Q_TILES):
-            nc.vector.tensor_reduce(result[:, :, qt * places : (qt + 1) * places], owned[qt], AXIS.X, ALU.add)
+                product(o[:, t, :], v_mx, slice(t * P, (t + 1) * P), w_mx[qt], slice(0, P))
+            nc.vector.tensor_tensor(owned[:, :, q_cols[qt]], o[:], own_sb[:, :, q_cols[qt]], ALU.mult)
+            places = slice(qt * P // HEADS, (qt + 1) * P // HEADS)
+            nc.vector.tensor_reduce(
+                result[:, :, places], owned[:, :, q_cols[qt]].rearrange("p t (x j) -> p t x j", j=HEADS), AXIS.X, ALU.add
+            )
         nc.sync.dma_start(out=out.rearrange("(p t) x -> p t x", t=PACK), in_=result[:])

@@ -97,7 +97,8 @@ def tile_attend_ownlists_gatedkeys_kernel(tc, query, keys, kgate, size, vals, ow
 
         km = [sb.tile([P, 2, I], F32, name="km" + str(pair)) for pair in range(2)]
         km_grouped = sb.tile([P, I * PACK + HALF], BF16, name="km_grouped", align_bytes=64)
-        km_view = km_grouped[:, 0 : I * PACK].rearrange("p (c i t) -> p c t i", i=4, t=PACK)
+        km_rows = km_grouped[:, HALF : HALF + I * PACK]
+        km_view = km_rows.rearrange("p (c i t) -> p c t i", i=4, t=PACK)
         gates = [sb.tile([P, I], F32, name="sig" + str(t)) for t in range(PACK)]
 
         def weave_keys(pair, slots):
@@ -122,9 +123,8 @@ def tile_attend_ownlists_gatedkeys_kernel(tc, query, keys, kgate, size, vals, ow
         v_grouped = sb.tile([P, PACK * I], BF16, name="v_grouped", tag="val0", align_bytes=64)
         w_rows = [sb.tile([P, I], BF16, name="w_rows" + str(qt), align_bytes=64)[:] for qt in range(Q_TILES)]
         picked = [sb.tile([P, I], BF16, name="picked" + str(t), align_bytes=64)[:] for t in (1, 2, 3)]
-        picked.insert(0, km_grouped[:, I * PACK - HALF : I * PACK + HALF])
+        picked.insert(0, km_grouped[:, 0:I])
         neg_max = [word(v_grouped, 2 * qt) for qt in range(Q_TILES)]
-        totals = sb.tile([P, Q_TILES], F32, name="totals")
 
         def pick(on_scalar, t, slots):
             if on_scalar:
@@ -149,31 +149,33 @@ def tile_attend_ownlists_gatedkeys_kernel(tc, query, keys, kgate, size, vals, ow
             out=q_grouped[:].rearrange("p (c i t) -> p c t i", i=4, t=PACK),
             in_=q_raw[:].rearrange("p t (c i) -> p c t i", i=4),
         )
-        km_mx = [mx_tiles(HALF, "km0"), mx_tiles(HALF, "km1", "q_grouped")]
         q_mx = mx_tiles(Q, "q")
-        quantize(km_mx[0], lower, km_grouped[:, 0 : HALF * PACK])
         quantize(q_mx, slice(0, Q), q_grouped[:])
-        quantize(km_mx[1], lower, km_grouped[:, HALF * PACK : I * PACK])
+        km_mx = mx_tiles(I, "km", "q_raw")
+        for slots in (lower, upper):
+            quantize(km_mx, slots, km_rows[:, slots.start * PACK : slots.stop * PACK])
 
         scores = [ps.tile([P, I], F32, name="score", tag="score" + str(qt)) for qt in range(Q_TILES)]
-        for h, slots in enumerate((lower, upper)):
-            for qt in range(Q_TILES):
-                product(scores[qt][:, slots], q_mx, q_cols[qt], km_mx[h], lower)
+        for qt in range(Q_TILES):
+            for slots in (lower, upper):
+                product(scores[qt][:, slots], q_mx, q_cols[qt], km_mx, slots)
 
-        pick(True, 0, upper)
-        pick(False, 0, lower)
+        pick(True, 0, lower)
+        pick(False, 0, upper)
         pick(True, 1, every)
         pick(True, 2, every)
         for t in range(3):
             turn_values(t)
 
-        probs = sb.tile([P, Q_TILES * I], F32, name="probs", tag="val2", align_bytes=64)
-        inv0 = sb.tile([P, Q_TILES], F32, name="inv0", tag="val3", align_bytes=64)
+        first = sb.tile([P, I + Q_TILES], F32, name="first", tag="val2", align_bytes=64)
+        second = sb.tile([P, I], F32, name="second")
+        probs, totals = [first[:, 0:I], second[:]], first[:, I : I + Q_TILES]
+        inv0 = sb.tile([P, Q_TILES], F32, name="inv0")
         inv = [inv0[:, qt : qt + 1] for qt in range(Q_TILES)]
         for qt in range(Q_TILES):
             nc.vector.tensor_reduce(neg_max[qt], scores[qt][:], AXIS.X, ALU.max, negate=True)
             nc.scalar.activation(
-                probs[:, qt * I : (qt + 1) * I].rearrange("p (u s e) -> p u s e", u=2, e=2),
+                probs[qt].rearrange("p (u s e) -> p u s e", u=2, e=2),
                 scores[qt][:].rearrange("p (s u e) -> p u s e", u=2, e=2),
                 ACT.Exp, bias=neg_max[qt], accum_out=totals[:, qt : qt + 1],
             )
@@ -187,7 +189,7 @@ def tile_attend_ownlists_gatedkeys_kernel(tc, query, keys, kgate, size, vals, ow
         w_turned = []
         for qt in range(Q_TILES):
             nc.vector.scalar_tensor_tensor(
-                w_rows[qt], probs[:, qt * I : (qt + 1) * I], inv[qt], size_all[:], ALU.mult, ALU.mult
+                w_rows[qt], probs[qt], inv[qt], size_all[:], ALU.mult, ALU.mult
             )
             turned = ps.tile([P, 1, 2, P], F32, name="w_turned", tag="score" + str(qt))
             for u in range(2):

@@ -188,30 +188,31 @@ def tile_attend_ownlists_gatedkeys_kernel(tc, query, keys, kgate, size, vals, ow
 
         w_turned = []
         for qt in range(Q_TILES):
-            nc.vector.scalar_tensor_tensor(
-                w_rows[qt], probs[qt], inv[qt], size_all[:], ALU.mult, ALU.mult
-            )
+            for slots in (every,) if qt == 0 else (lower, upper):
+                nc.vector.scalar_tensor_tensor(
+                    w_rows[qt][:, slots], probs[qt][:, slots], inv[qt], size_all[:, slots], ALU.mult, ALU.mult
+                )
             turned = ps.tile([P, 1, 2, P], F32, name="w_turned", tag="score" + str(qt))
             for u in range(2):
                 nc.tensor.transpose(turned[:, 0, u, :], w_rows[qt].bitcast(F32)[:, u * P : (u + 1) * P], ident[:])
             w_turned.append(turned)
 
         w_grouped = sb.tile([P, Q * PACK], BF16, name="w_grouped", align_bytes=64)
-        v_mx = mx_tiles(PACK * P, "v", "val2")
-        quantize(v_mx, slice(0, 2 * P), v_grouped[:, 0 : 2 * I])
+        v_mx = [mx_tiles(2 * P, "v01", "val2"), mx_tiles(2 * P, "v23", "w_rows1")]
+        quantize(v_mx[0], slice(0, 2 * P), v_grouped[:, 0 : 2 * I])
         w_mx = [mx_tiles(P, "w" + str(qt)) for qt in range(Q_TILES)]
         for qt in range(Q_TILES):
             group(nc.scalar.copy, w_turned[qt], w_grouped[:, qt * I : (qt + 1) * I])
             quantize(w_mx[qt], slice(0, P), w_grouped[:, qt * I : (qt + 1) * I])
             if qt == 0:
-                quantize(v_mx, slice(2 * P, 4 * P), v_grouped[:, 2 * I : 4 * I])
+                quantize(v_mx[1], slice(0, 2 * P), v_grouped[:, 2 * I : 4 * I])
 
         result = sb.tile([P, PACK, X], F32, name="result", align_bytes=64)
-        owned = sb.tile([P, PACK, Q], F32, name="owned", tag="w_grouped", align_bytes=64)
+        owned = sb.tile([P, PACK, Q], F32, name="owned")
         for qt in range(Q_TILES):
             o = ps.tile([P, PACK, P], F32, name="o", tag="out" + str(qt))
             for t in range(PACK):
-                product(o[:, t, :], v_mx, slice(t * P, (t + 1) * P), w_mx[qt], slice(0, P))
+                product(o[:, t, :], v_mx[t // 2], slice(t % 2 * P, (t % 2 + 1) * P), w_mx[qt], slice(0, P))
             nc.vector.tensor_tensor(owned[:, :, q_cols[qt]], o[:], own_sb[:, :, q_cols[qt]], ALU.mult)
             places = slice(qt * P // HEADS, (qt + 1) * P // HEADS)
             nc.vector.tensor_reduce(

@@ -62,7 +62,11 @@ def tile_attend_ownlists_gatedkeys_kernel(tc, query, keys, kgate, size, vals, ow
 
         gate_pl, key_pl, val_pl = plane_tiles("gate"), plane_tiles("key"), plane_tiles("val")
         size_col = sb.tile([P, PACK], F32, name="size_col")
-        nc.scalar.dma_start(out=size_col[:], in_=size.rearrange("o (p t) -> (o p) t", t=PACK))
+        for u in range(2):
+            nc.scalar.dma_start(
+                out=size_col[u * 64 : (u + 1) * 64, :].rearrange("p (s e) -> p s e", e=2),
+                in_=size.rearrange("o (p s u e) -> (o p) s u e", s=2, u=2, e=2)[:, :, u, :],
+            )
         load_plane(gate_pl, kgate, 0)
         nc.sync.dma_start(offsets[:], offs)
         load_plane(key_pl, keys, 0)
@@ -81,19 +85,12 @@ def tile_attend_ownlists_gatedkeys_kernel(tc, query, keys, kgate, size, vals, ow
         ident = sb.tile([P, P], F32, name="ident")
         make_identity(nc, ident[:])
 
-        warm = sb.tile([P, 8], F32, name="warm")
-        nc.vector.memset(warm[:], 0.0)
         warm_out = sb.tile([P, 8], F32, name="warm_out")
-        nc.scalar.activation(warm_out[:], warm[:], ACT.Sigmoid)
 
-        size_turned = ps.tile([P, PACK, P], F32, name="size_turned", tag="out0")
+        size_turned = ps.tile([P, PACK, P], F32, name="size_turned")
         for t in range(PACK):
             nc.tensor.transpose(size_turned[:, t, :], size_col[:, t : t + 1].to_broadcast([P, P]), ident[:])
-        size_all = sb.tile([P, I], F32, name="size_all", align_bytes=64)
-        nc.vector.tensor_copy(
-            out=size_all[:].rearrange("p (u s e) -> p u s e", u=2, e=2),
-            in_=size_turned[:].rearrange("p (u e) s -> p u s e", u=2),
-        )
+        size_all = size_turned[:].rearrange("p t s -> p s t")
 
         km = [sb.tile([P, 2, I], F32, name="km" + str(pair)) for pair in range(2)]
         km_grouped = sb.tile([P, I * PACK + HALF], BF16, name="km_grouped", align_bytes=64)
@@ -190,7 +187,9 @@ def tile_attend_ownlists_gatedkeys_kernel(tc, query, keys, kgate, size, vals, ow
         for qt in range(Q_TILES):
             for slots in (every,) if qt == 0 else (lower, upper):
                 nc.vector.scalar_tensor_tensor(
-                    w_rows[qt][:, slots], probs[qt][:, slots], inv[qt], size_all[:, slots], ALU.mult, ALU.mult
+                    w_rows[qt][:, slots].rearrange("p (s t) -> p s t", t=PACK),
+                    probs[qt][:, slots].rearrange("p (s t) -> p s t", t=PACK),
+                    inv[qt], size_all[:, slots.start // PACK : slots.stop // PACK, :], ALU.mult, ALU.mult,
                 )
             turned = ps.tile([P, 1, 2, P], F32, name="w_turned", tag="score" + str(qt))
             for u in range(2):

@@ -93,8 +93,8 @@ def tile_attend_ownlists_gatedkeys_kernel(tc, query, keys, kgate, size, vals, ow
         size_all = size_turned[:].rearrange("p t s -> p s t")
 
         km = [sb.tile([P, 2, I], F32, name="km" + str(pair)) for pair in range(2)]
-        km_grouped = sb.tile([P, I * PACK + HALF], BF16, name="km_grouped", align_bytes=64)
-        km_rows = km_grouped[:, HALF : HALF + I * PACK]
+        km_grouped = sb.tile([P, I * PACK], BF16, name="km_grouped", align_bytes=64)
+        km_rows = km_grouped[:]
         km_view = km_rows.rearrange("p (c i t) -> p c t i", i=4, t=PACK)
         gates = [sb.tile([P, I], F32, name="sig" + str(t)) for t in range(PACK)]
 
@@ -117,11 +117,9 @@ def tile_attend_ownlists_gatedkeys_kernel(tc, query, keys, kgate, size, vals, ow
         weave_keys(1, upper)
 
         q_grouped = sb.tile([P, Q * PACK], BF16, name="q_grouped", align_bytes=64)
-        v_grouped = sb.tile([P, PACK * I], BF16, name="v_grouped", tag="val0", align_bytes=64)
+        picked = [sb.tile([P, I], BF16, name="picked" + str(t), align_bytes=64)[:] for t in range(PACK)]
         w_rows = [sb.tile([P, I], BF16, name="w_rows" + str(qt), align_bytes=64)[:] for qt in range(Q_TILES)]
-        picked = [sb.tile([P, I], BF16, name="picked" + str(t), align_bytes=64)[:] for t in (1, 2, 3)]
-        picked.insert(0, km_grouped[:, 0:I])
-        neg_max = [word(v_grouped, 2 * qt) for qt in range(Q_TILES)]
+        neg_max = [sb.tile([P, 1], F32, name="neg_max" + str(qt))[:] for qt in range(Q_TILES)]
 
         def pick(on_scalar, t, slots):
             if on_scalar:
@@ -129,92 +127,117 @@ def tile_attend_ownlists_gatedkeys_kernel(tc, query, keys, kgate, size, vals, ow
             else:
                 nc.vector.tensor_copy(picked[t][:, slots], listed(val_pl[t], slots))
 
-        v_turned = [ps.tile([P, 2, 2, P], F32, name="v_turned" + str(pair)) for pair in range(2)]
-
-        def turn_values(t):
+        def turn_values(t, bank):
             words = picked[t].bitcast(F32)
             for u in range(2):
-                nc.tensor.transpose(v_turned[t // 2][:, t % 2, u, :], words[:, u : I // 2 : 2], ident[:])
+                nc.tensor.transpose(bank[:, u, :], words[:, u : I // 2 : 2], ident[:])
 
         def group(copy, turned, grouped):
             copy(
                 out=grouped.bitcast(F32).rearrange("p (k m u) -> p k m u", m=P, u=2),
-                in_=turned[:].rearrange("p k u m -> p k m u"),
+                in_=turned.rearrange("p k u m -> p k m u"),
             )
 
-        nc.scalar.copy(
-            out=q_grouped[:].rearrange("p (c i t) -> p c t i", i=4, t=PACK),
-            in_=q_raw[:].rearrange("p t (c i) -> p c t i", i=4),
-        )
         q_mx = mx_tiles(Q, "q")
-        quantize(q_mx, slice(0, Q), q_grouped[:])
-        km_mx = mx_tiles(I, "km", "q_raw")
-        for slots in (lower, upper):
-            quantize(km_mx, slots, km_rows[:, slots.start * PACK : slots.stop * PACK])
+        km_mx = [mx_tiles(HALF, "km0"), mx_tiles(HALF, "km1", "q_raw")]
+        for qt in range(Q_TILES):
+            nc.scalar.copy(
+                out=q_grouped[:, qt * I : (qt + 1) * I].rearrange("p (c i t) -> p c t i", i=4, t=PACK),
+                in_=q_raw[:, :, q_cols[qt]].rearrange("p t (c i) -> p c t i", i=4),
+            )
+        for half in range(2):
+            quantize(km_mx[half], lower, km_rows[:, half * HALF * PACK : (half + 1) * HALF * PACK])
+            quantize(q_mx, q_cols[half], q_grouped[:, half * I : (half + 1) * I])
 
         scores = [ps.tile([P, I], F32, name="score", tag="score" + str(qt)) for qt in range(Q_TILES)]
         for qt in range(Q_TILES):
-            for slots in (lower, upper):
-                product(scores[qt][:, slots], q_mx, q_cols[qt], km_mx, slots)
+            for half, slots in enumerate((lower, upper)):
+                product(scores[qt][:, slots], q_mx, q_cols[qt], km_mx[half], lower)
 
-        pick(True, 0, lower)
-        pick(False, 0, upper)
+        pick(True, 0, every)
         pick(True, 1, every)
-        pick(True, 2, every)
-        for t in range(3):
-            turn_values(t)
 
-        first = sb.tile([P, I + Q_TILES], F32, name="first", tag="val2", align_bytes=64)
-        second = sb.tile([P, I], F32, name="second")
-        probs, totals = [first[:, 0:I], second[:]], first[:, I : I + Q_TILES]
-        inv0 = sb.tile([P, Q_TILES], F32, name="inv0")
-        inv = [inv0[:, qt : qt + 1] for qt in range(Q_TILES)]
+        probs = [sb.tile([P, I], F32, name="probs" + str(qt))[:] for qt in range(Q_TILES)]
+        totals = [sb.tile([P, 1], F32, name="total" + str(qt))[:] for qt in range(Q_TILES)]
+        inv = [sb.tile([P, 1], F32, name="inv" + str(qt))[:] for qt in range(Q_TILES)]
         for qt in range(Q_TILES):
             nc.vector.tensor_reduce(neg_max[qt], scores[qt][:], AXIS.X, ALU.max, negate=True)
             nc.scalar.activation(
                 probs[qt].rearrange("p (u s e) -> p u s e", u=2, e=2),
                 scores[qt][:].rearrange("p (s u e) -> p u s e", u=2, e=2),
-                ACT.Exp, bias=neg_max[qt], accum_out=totals[:, qt : qt + 1],
+                ACT.Exp, bias=neg_max[qt], accum_out=totals[qt],
             )
-        pick(False, 3, every)
-        for qt in range(Q_TILES):
-            nc.vector.reciprocal(inv[qt], totals[:, qt : qt + 1])
-        turn_values(3)
-        for pair in range(2):
-            group(nc.scalar.copy, v_turned[pair], v_grouped[:, pair * 2 * I : (pair + 1) * 2 * I])
 
-        w_turned = []
+        def weigh(qt, slots):
+            nc.vector.scalar_tensor_tensor(
+                w_rows[qt][:, slots].rearrange("p (s t) -> p s t", t=PACK),
+                probs[qt][:, slots].rearrange("p (s t) -> p s t", t=PACK),
+                inv[qt], size_all[:, slots.start // PACK : slots.stop // PACK, :], ALU.mult, ALU.mult,
+            )
+
+        v01_turned = ps.tile([P, 2, 2, P], F32, name="v01_turned", tag="score0")
+        for t in range(2):
+            turn_values(t, v01_turned[:, t])
+        pick(False, 2, upper)
+        nc.vector.reciprocal(inv[0], totals[0])
+        weigh(0, lower)
+        nc.vector.reciprocal(inv[1], totals[1])
+        weigh(0, upper)
+        weigh(1, every)
+        pick(True, 2, lower)
+        w_turned = [ps.tile([P, 1, 2, P], F32, name="w_turned", tag=tag) for tag in ("score1", "w1")]
         for qt in range(Q_TILES):
-            for slots in (every,) if qt == 0 else (lower, upper):
-                nc.vector.scalar_tensor_tensor(
-                    w_rows[qt][:, slots].rearrange("p (s t) -> p s t", t=PACK),
-                    probs[qt][:, slots].rearrange("p (s t) -> p s t", t=PACK),
-                    inv[qt], size_all[:, slots.start // PACK : slots.stop // PACK, :], ALU.mult, ALU.mult,
-                )
-            turned = ps.tile([P, 1, 2, P], F32, name="w_turned", tag="score" + str(qt))
             for u in range(2):
-                nc.tensor.transpose(turned[:, 0, u, :], w_rows[qt].bitcast(F32)[:, u * P : (u + 1) * P], ident[:])
-            w_turned.append(turned)
+                nc.tensor.transpose(w_turned[qt][:, 0, u, :], w_rows[qt].bitcast(F32)[:, u * P : (u + 1) * P], ident[:])
 
-        w_grouped = sb.tile([P, Q * PACK], BF16, name="w_grouped", align_bytes=64)
-        v_mx = [mx_tiles(2 * P, "v01", "val2"), mx_tiles(2 * P, "v23", "w_rows1")]
-        quantize(v_mx[0], slice(0, 2 * P), v_grouped[:, 0 : 2 * I])
-        w_mx = [mx_tiles(P, "w" + str(qt)) for qt in range(Q_TILES)]
+        v_grouped = sb.tile([P, PACK * I], BF16, name="v_grouped", align_bytes=64)
+        w_grouped = [sb.tile([P, I], BF16, name="w_grouped" + str(qt), align_bytes=64)[:] for qt in range(Q_TILES)]
+        w_mx = mx_tiles(Q, "w")
+        v01_mx = mx_tiles(2 * P, "v01")
+        group(nc.scalar.copy, v01_turned[:], v_grouped[:, 0 : 2 * I])
+        pick(True, 3, every)
+        group(nc.vector.tensor_copy, w_turned[0][:], w_grouped[0])
+        for t, tag in ((2, "score1"), (3, "v3")):
+            turned = ps.tile([P, 1, 2, P], F32, name="v_turned", tag=tag)
+            turn_values(t, turned[:, 0])
+            group(nc.scalar.copy, turned[:], v_grouped[:, t * I : (t + 1) * I])
+
+        quantize(v01_mx, slice(0, 2 * P), v_grouped[:, 0 : 2 * I])
+        group(nc.vector.tensor_copy, w_turned[1][:], w_grouped[1])
         for qt in range(Q_TILES):
-            group(nc.scalar.copy, w_turned[qt], w_grouped[:, qt * I : (qt + 1) * I])
-            quantize(w_mx[qt], slice(0, P), w_grouped[:, qt * I : (qt + 1) * I])
-            if qt == 0:
-                quantize(v_mx[1], slice(0, 2 * P), v_grouped[:, 2 * I : 4 * I])
+            quantize(w_mx, q_cols[qt], w_grouped[qt])
 
         result = sb.tile([P, PACK, X], F32, name="result", align_bytes=64)
-        owned = sb.tile([P, PACK, Q], F32, name="owned")
-        for qt in range(Q_TILES):
-            o = ps.tile([P, PACK, P], F32, name="o", tag="out" + str(qt))
-            for t in range(PACK):
-                product(o[:, t, :], v_mx[t // 2], slice(t % 2 * P, (t % 2 + 1) * P), w_mx[qt], slice(0, P))
-            nc.vector.tensor_tensor(owned[:, :, q_cols[qt]], o[:], own_sb[:, :, q_cols[qt]], ALU.mult)
-            places = slice(qt * P // HEADS, (qt + 1) * P // HEADS)
-            nc.vector.tensor_reduce(
-                result[:, :, places], owned[:, :, q_cols[qt]].rearrange("p t (x j) -> p t x j", j=HEADS), AXIS.X, ALU.add
+        owned = sb.tile([P, PACK * Q], F32, name="owned")
+        o = [ps.tile([P, 2, Q], F32, name="o" + str(pair)) for pair in range(2)]
+
+        v_mx = [(v01_mx, 0), (v01_mx, P), (mx_tiles(P, "v2", "w_grouped0"), 0), (mx_tiles(P, "v3"), 0)]
+
+        def multiply(t):
+            mx, col = v_mx[t]
+            product(o[t // 2][:, t % 2, :], mx, slice(col, col + P), w_mx, slice(0, Q))
+
+        def keep_own(pair):
+            nc.vector.tensor_tensor(
+                owned[:, pair * 2 * Q : (pair + 1) * 2 * Q].rearrange("p (t q) -> p t q", t=2),
+                o[pair][:], own_sb[:, 2 * pair : 2 * pair + 2, :], ALU.mult,
             )
+
+        def sum_heads(pair):
+            nc.vector.tensor_reduce(
+                result[:, 2 * pair : 2 * pair + 2, :],
+                owned[:, pair * 2 * Q : (pair + 1) * 2 * Q].rearrange("p (t x j) -> p t x j", t=2, j=HEADS),
+                AXIS.X, ALU.add,
+            )
+
+        multiply(0)
+        multiply(1)
+        quantize(v_mx[2][0], slice(0, P), v_grouped[:, 2 * I : 3 * I])
+        quantize(v_mx[3][0], slice(0, P), v_grouped[:, 3 * I : 4 * I])
+        multiply(2)
+        multiply(3)
+        keep_own(0)
+        keep_own(1)
+        sum_heads(0)
+        sum_heads(1)
         nc.sync.dma_start(out=out.rearrange("(p t) x -> p t x", t=PACK), in_=result[:])

@@ -62,11 +62,7 @@ def tile_attend_ownlists_gatedkeys_kernel(tc, query, keys, kgate, size, vals, ow
 
         gate_pl, key_pl, val_pl = plane_tiles("gate"), plane_tiles("key"), plane_tiles("val")
         size_col = sb.tile([P, PACK], F32, name="size_col")
-        for u in range(2):
-            nc.scalar.dma_start(
-                out=size_col[u * 64 : (u + 1) * 64, :].rearrange("p (s e) -> p s e", e=2),
-                in_=size.rearrange("o (p s u e) -> (o p) s u e", s=2, u=2, e=2)[:, :, u, :],
-            )
+        nc.scalar.dma_start(out=size_col[:], in_=size.rearrange("o (p t) -> (o p) t", t=PACK))
         load_plane(gate_pl, kgate, 0)
         nc.sync.dma_start(offsets[:], offs)
         load_plane(key_pl, keys, 0)
@@ -90,7 +86,6 @@ def tile_attend_ownlists_gatedkeys_kernel(tc, query, keys, kgate, size, vals, ow
         size_turned = ps.tile([P, PACK, P], F32, name="size_turned")
         for t in range(PACK):
             nc.tensor.transpose(size_turned[:, t, :], size_col[:, t : t + 1].to_broadcast([P, P]), ident[:])
-        size_all = size_turned[:].rearrange("p t s -> p s t")
 
         km = [sb.tile([P, 2, I], F32, name="km" + str(pair)) for pair in range(2)]
         km_grouped = sb.tile([P, I * PACK], BF16, name="km_grouped", align_bytes=64)
@@ -168,11 +163,12 @@ def tile_attend_ownlists_gatedkeys_kernel(tc, query, keys, kgate, size, vals, ow
                 ACT.Exp, bias=neg_max[qt], accum_out=totals[qt],
             )
 
-        def weigh(qt, slots):
+        def weigh(qt, u):
+            places = slice(u * HALF, (u + 1) * HALF)
             nc.vector.scalar_tensor_tensor(
-                w_rows[qt][:, slots].rearrange("p (s t) -> p s t", t=PACK),
-                probs[qt][:, slots].rearrange("p (s t) -> p s t", t=PACK),
-                inv[qt], size_all[:, slots.start // PACK : slots.stop // PACK, :], ALU.mult, ALU.mult,
+                w_rows[qt][:, places].rearrange("p (s e) -> p s e", e=2),
+                probs[qt][:, places].rearrange("p (s e) -> p s e", e=2),
+                inv[qt], size_turned[:, 2 * u : 2 * u + 2, :].rearrange("p e s -> p s e"), ALU.mult, ALU.mult,
             )
 
         v01_turned = ps.tile([P, 2, 2, P], F32, name="v01_turned", tag="score0")
@@ -180,10 +176,11 @@ def tile_attend_ownlists_gatedkeys_kernel(tc, query, keys, kgate, size, vals, ow
             turn_values(t, v01_turned[:, t])
         pick(False, 2, upper)
         nc.vector.reciprocal(inv[0], totals[0])
-        weigh(0, lower)
+        weigh(0, 0)
         nc.vector.reciprocal(inv[1], totals[1])
-        weigh(0, upper)
-        weigh(1, every)
+        weigh(0, 1)
+        weigh(1, 0)
+        weigh(1, 1)
         pick(True, 2, lower)
         w_turned = [ps.tile([P, 1, 2, P], F32, name="w_turned", tag=tag) for tag in ("score1", "w1")]
         for qt in range(Q_TILES):

@@ -233,8 +233,21 @@ def tile_attend_ownlists_gatedkeys_kernel(tc, query, keys, kgate, size, vals, ow
         quantize(v_mx[3][0], slice(0, P), v_grouped[:, 3 * I : 4 * I])
         multiply(2)
         multiply(3)
-        keep_own(0)
-        keep_own(1)
-        sum_heads(0)
-        sum_heads(1)
+        split = sb.tile([P, 2, Q], F32, name="split")
+        halves = sb.tile([P, Q], F32, name="halves")
+        nc.vector.tensor_tensor(
+            split[:].rearrange("p h (c i) -> p c h i", i=4),
+            o[0][:].rearrange("p t (x h i) -> p (t x) h i", h=2, i=4),
+            own_sb[:, 0:2, :].rearrange("p t (x h i) -> p (t x) h i", h=2, i=4), ALU.mult,
+        )
+        nc.gpsimd.tensor_tensor(halves[:], split[:, 0, :], split[:, 1, :], ALU.add)
+        for t in (2, 3):
+            nc.vector.tensor_tensor(owned[:, t * Q : (t + 1) * Q], o[1][:, t - 2, :], own_sb[:, t, :], ALU.mult)
+        for t in (2, 3):
+            nc.vector.tensor_reduce(
+                result[:, t, :], owned[:, t * Q : (t + 1) * Q].rearrange("p (x j) -> p x j", j=HEADS), AXIS.X, ALU.add
+            )
+        nc.vector.tensor_reduce(
+            result[:, 0:2, :], halves[:].rearrange("p (t x i) -> p t x i", t=2, i=4), AXIS.X, ALU.add
+        )
         nc.sync.dma_start(out=out.rearrange("(p t) x -> p t x", t=PACK), in_=result[:])

@@ -112,9 +112,10 @@ def tile_attend_ownlists_gatedkeys_kernel(tc, query, keys, kgate, size, vals, ow
         weave_keys(1, upper)
 
         q_grouped = sb.tile([P, Q * PACK], BF16, name="q_grouped", align_bytes=64)
-        picked = [sb.tile([P, I], BF16, name="picked" + str(t), align_bytes=64)[:] for t in range(PACK)]
+        picked = [sb.tile([P, I], BF16, name="picked" + str(t), align_bytes=64)[:] for t in range(PACK - 1)]
         w_rows = [sb.tile([P, I], BF16, name="w_rows" + str(qt), align_bytes=64)[:] for qt in range(Q_TILES)]
-        neg_max = [sb.tile([P, 1], F32, name="neg_max" + str(qt))[:] for qt in range(Q_TILES)]
+        v_grouped = sb.tile([P, PACK * I], BF16, name="v_grouped", align_bytes=64)
+        neg_max = [sb.tile([P, 1], F32, name="neg_max0")[:], v_grouped[:, 0:2].bitcast(F32)]
 
         def pick(on_scalar, t, slots):
             if on_scalar:
@@ -171,7 +172,7 @@ def tile_attend_ownlists_gatedkeys_kernel(tc, query, keys, kgate, size, vals, ow
                 inv[qt], size_turned[:, 2 * u : 2 * u + 2, :].rearrange("p e s -> p s e"), ALU.mult, ALU.mult,
             )
 
-        v01_turned = ps.tile([P, 2, 2, P], F32, name="v01_turned", tag="score0")
+        v01_turned = ps.tile([P, 2, 2, P], F32, name="v01_turned")
         for t in range(2):
             turn_values(t, v01_turned[:, t])
         pick(False, 2, upper)
@@ -182,19 +183,19 @@ def tile_attend_ownlists_gatedkeys_kernel(tc, query, keys, kgate, size, vals, ow
         weigh(1, 0)
         weigh(1, 1)
         pick(True, 2, lower)
-        w_turned = [ps.tile([P, 1, 2, P], F32, name="w_turned", tag=tag) for tag in ("score1", "w1")]
+        w_turned = [ps.tile([P, 1, 2, P], F32, name="w_turned", tag=tag) for tag in ("score0", "score1")]
         for qt in range(Q_TILES):
             for u in range(2):
                 nc.tensor.transpose(w_turned[qt][:, 0, u, :], w_rows[qt].bitcast(F32)[:, u * P : (u + 1) * P], ident[:])
 
-        v_grouped = sb.tile([P, PACK * I], BF16, name="v_grouped", align_bytes=64)
         w_grouped = [sb.tile([P, I], BF16, name="w_grouped" + str(qt), align_bytes=64)[:] for qt in range(Q_TILES)]
         w_mx = mx_tiles(Q, "w")
         v01_mx = mx_tiles(2 * P, "v01")
         group(nc.scalar.copy, v01_turned[:], v_grouped[:, 0 : 2 * I])
+        picked.append(probs[0][:, HALF:I].bitcast(BF16))
         pick(True, 3, every)
         group(nc.vector.tensor_copy, w_turned[0][:], w_grouped[0])
-        for t, tag in ((2, "score1"), (3, "v3")):
+        for t, tag in ((2, "score0"), (3, "v3")):
             turned = ps.tile([P, 1, 2, P], F32, name="v_turned", tag=tag)
             turn_values(t, turned[:, 0])
             group(nc.scalar.copy, turned[:], v_grouped[:, t * I : (t + 1) * I])

@@ -206,49 +206,40 @@ def tile_attend_ownlists_gatedkeys_kernel(tc, query, keys, kgate, size, vals, ow
             quantize(w_mx, q_cols[qt], w_grouped[qt])
 
         result = sb.tile([P, PACK, X], F32, name="result", align_bytes=64)
-        owned = sb.tile([P, PACK * Q], F32, name="owned")
-        o = [ps.tile([P, 2, Q], F32, name="o" + str(pair)) for pair in range(2)]
-
-        v_mx = [(v01_mx, 0), (v01_mx, P), (mx_tiles(P, "v2", "w_grouped0"), 0), (mx_tiles(P, "v3"), 0)]
-
-        def multiply(t):
-            mx, col = v_mx[t]
-            product(o[t // 2][:, t % 2, :], mx, slice(col, col + P), w_mx, slice(0, Q))
-
-        def keep_own(pair):
-            nc.vector.tensor_tensor(
-                owned[:, pair * 2 * Q : (pair + 1) * 2 * Q].rearrange("p (t q) -> p t q", t=2),
-                o[pair][:], own_sb[:, 2 * pair : 2 * pair + 2, :], ALU.mult,
-            )
-
-        def sum_heads(pair):
-            nc.vector.tensor_reduce(
-                result[:, 2 * pair : 2 * pair + 2, :],
-                owned[:, pair * 2 * Q : (pair + 1) * 2 * Q].rearrange("p (t x j) -> p t x j", t=2, j=HEADS),
-                AXIS.X, ALU.add,
-            )
-
-        multiply(0)
-        multiply(1)
-        quantize(v_mx[2][0], slice(0, P), v_grouped[:, 2 * I : 3 * I])
-        quantize(v_mx[3][0], slice(0, P), v_grouped[:, 3 * I : 4 * I])
-        multiply(2)
-        multiply(3)
+        owned = sb.tile([P, 2, Q], F32, name="owned")
         split = sb.tile([P, 2, Q], F32, name="split")
         halves = sb.tile([P, Q], F32, name="halves")
-        nc.vector.tensor_tensor(
-            split[:].rearrange("p h (c i) -> p c h i", i=4),
-            o[0][:].rearrange("p t (x h i) -> p (t x) h i", h=2, i=4),
-            own_sb[:, 0:2, :].rearrange("p t (x h i) -> p (t x) h i", h=2, i=4), ALU.mult,
-        )
+        early = [ps.tile([P, Q], F32, name="o" + str(t)) for t in range(2)]
+        late = ps.tile([P, 2, Q], F32, name="o23")
+        late_mx = {2: mx_tiles(P, "v2", "w_grouped0"), 3: mx_tiles(P, "v3")}
+
+        def by_halves(ap):
+            return ap.rearrange("p (x h i) -> p x h i", h=2, i=4)
+
+        def keep_own_split(t):
+            nc.vector.tensor_tensor(
+                split[:, :, t * P : (t + 1) * P].rearrange("p h (x i) -> p x h i", i=4),
+                by_halves(early[t][:]), by_halves(own_sb[:, t, :]), ALU.mult,
+            )
+
+        for t in range(2):
+            product(early[t][:], v01_mx, slice(t * P, (t + 1) * P), w_mx, slice(0, Q))
+        quantize(late_mx[2], slice(0, P), v_grouped[:, 2 * I : 3 * I])
+        quantize(late_mx[3], slice(0, P), v_grouped[:, 3 * I : 4 * I])
+        keep_own_split(0)
+        for t in (2, 3):
+            product(late[:, t - 2, :], late_mx[t], slice(0, P), w_mx, slice(0, Q))
+        keep_own_split(1)
         nc.gpsimd.tensor_tensor(halves[:], split[:, 0, :], split[:, 1, :], ALU.add)
         for t in (2, 3):
-            nc.vector.tensor_tensor(owned[:, t * Q : (t + 1) * Q], o[1][:, t - 2, :], own_sb[:, t, :], ALU.mult)
+            nc.vector.tensor_tensor(owned[:, t - 2, :], late[:, t - 2, :], own_sb[:, t, :], ALU.mult)
         for t in (2, 3):
             nc.vector.tensor_reduce(
-                result[:, t, :], owned[:, t * Q : (t + 1) * Q].rearrange("p (x j) -> p x j", j=HEADS), AXIS.X, ALU.add
+                result[:, t, :], owned[:, t - 2, :].rearrange("p (x j) -> p x j", j=HEADS), AXIS.X, ALU.add
             )
+        out_planes = out.rearrange("(p t) x -> p t x", t=PACK)
+        nc.scalar.dma_start(out=out_planes[:, 2:4, :], in_=result[:, 2:4, :])
         nc.vector.tensor_reduce(
             result[:, 0:2, :], halves[:].rearrange("p (t x i) -> p t x i", t=2, i=4), AXIS.X, ALU.add
         )
-        nc.sync.dma_start(out=out.rearrange("(p t) x -> p t x", t=PACK), in_=result[:])
+        nc.sync.dma_start(out=out_planes[:, 0:2, :], in_=result[:, 0:2, :])

@@ -210,7 +210,7 @@ def tile_attend_ownlists_gatedkeys_kernel(tc, query, keys, kgate, size, vals, ow
         split = sb.tile([P, 2, Q], F32, name="split")
         halves = sb.tile([P, Q], F32, name="halves")
         early = [ps.tile([P, Q], F32, name="o" + str(t)) for t in range(2)]
-        late = ps.tile([P, 2, Q], F32, name="o23")
+        late = {t: ps.tile([P, Q], F32, name="o" + str(t), tag=tag) for t, tag in ((2, "v01_turned"), (3, "o3"))}
         late_mx = {2: mx_tiles(P, "v2", "w_grouped0"), 3: mx_tiles(P, "v3")}
 
         def by_halves(ap):
@@ -228,11 +228,11 @@ def tile_attend_ownlists_gatedkeys_kernel(tc, query, keys, kgate, size, vals, ow
         quantize(late_mx[3], slice(0, P), v_grouped[:, 3 * I : 4 * I])
         keep_own_split(0)
         for t in (2, 3):
-            product(late[:, t - 2, :], late_mx[t], slice(0, P), w_mx, slice(0, Q))
+            product(late[t][:], late_mx[t], slice(0, P), w_mx, slice(0, Q))
         keep_own_split(1)
         nc.gpsimd.tensor_tensor(halves[:], split[:, 0, :], split[:, 1, :], ALU.add)
         for t in (2, 3):
-            nc.vector.tensor_tensor(owned[:, t - 2, :], late[:, t - 2, :], own_sb[:, t, :], ALU.mult)
+            nc.vector.tensor_tensor(owned[:, t - 2, :], late[t][:], own_sb[:, t, :], ALU.mult)
         for t in (2, 3):
             nc.vector.tensor_reduce(
                 result[:, t, :], owned[:, t - 2, :].rearrange("p (x j) -> p x j", j=HEADS), AXIS.X, ALU.add

@@ -29,8 +29,8 @@ def tile_attend_ownlists_gatedkeys_kernel(tc, query, keys, kgate, size, vals, ow
         sb = ctx.enter_context(tc.tile_pool(name="sb", bufs=1))
         ps = ctx.enter_context(tc.psum_pool(name="ps", bufs=1))
 
-        def mx_tiles(width, name, tag=""):
-            codes = sb.tile([P, width], U32, name=name + "_codes", tag=tag or name + "_codes", align_bytes=64)
+        def mx_tiles(width, name, tag="", align=64):
+            codes = sb.tile([P, width], U32, name=name + "_codes", tag=tag or name + "_codes", align_bytes=align)
             scales = sb.tile([P, width], U8, name=name + "_scales", align_bytes=64)
             return codes, scales
 
@@ -52,7 +52,7 @@ def tile_attend_ownlists_gatedkeys_kernel(tc, query, keys, kgate, size, vals, ow
             return plane[:].indirect(offsets[:, slots.start // 16 : slots.stop // 16])
 
         def plane_tiles(name):
-            return [sb.tile([P, T], F32, name=name + str(t), align_bytes=64) for t in range(PACK)]
+            return [sb.tile([P, T], F32, name=name + str(t), align_bytes=256) for t in range(PACK)]
 
         def load_plane(tiles, src, t):
             nc.sync.dma_start(out=tiles[t][:], in_=src.rearrange("(p t) n -> p t n", t=PACK)[:, t, :])
@@ -71,17 +71,18 @@ def tile_attend_ownlists_gatedkeys_kernel(tc, query, keys, kgate, size, vals, ow
         for tiles, src in ((gate_pl, kgate), (key_pl, keys)):
             for t in (2, 3):
                 load_plane(tiles, src, t)
-        q_raw = sb.tile([P, PACK, Q], F32, name="q_raw", align_bytes=64)
+        q_raw = sb.tile([P, PACK, Q], F32, name="q_raw", align_bytes=256)
         nc.sync.dma_start(out=q_raw[:], in_=query.rearrange("(p t) q -> p t q", t=PACK))
         for t in range(PACK):
             load_plane(val_pl, vals, t)
-        own_sb = sb.tile([P, PACK, Q], F32, name="own_sb")
+        own_sb = sb.tile([P, PACK, Q], F32, name="own_sb", align_bytes=256)
         nc.sync.dma_start(out=own_sb[:], in_=own.rearrange("(p t) q -> p t q", t=PACK))
 
         ident = sb.tile([P, P], F32, name="ident")
         make_identity(nc, ident[:])
 
-        warm_out = sb.tile([P, 8], F32, name="warm_out")
+        warm_in = sb.tile([P, 8], F32, name="warm_in")
+        nc.gpsimd.memset(warm_in[:], 0.0)
 
         size_turned = ps.tile([P, PACK, P], F32, name="size_turned")
         for t in range(PACK):
@@ -107,7 +108,8 @@ def tile_attend_ownlists_gatedkeys_kernel(tc, query, keys, kgate, size, vals, ow
                 )
             if t == 1:
                 weave_keys(0, every)
-        nc.scalar.activation(warm_out[:], gates[-1][:, 0:8], ACT.Exp)
+        warm_out = sb.tile([P, 8], F32, name="warm_out", tag="gate3", align_bytes=256)
+        nc.scalar.activation(warm_out[:], warm_in[:], ACT.Exp)
         weave_keys(1, lower)
         weave_keys(1, upper)
 
@@ -135,7 +137,7 @@ def tile_attend_ownlists_gatedkeys_kernel(tc, query, keys, kgate, size, vals, ow
             )
 
         q_mx = mx_tiles(Q, "q")
-        km_mx = [mx_tiles(HALF, "km0"), mx_tiles(HALF, "km1", "q_raw")]
+        km_mx = [mx_tiles(HALF, "km0"), mx_tiles(HALF, "km1", "q_raw", 256)]
         for qt in range(Q_TILES):
             nc.scalar.copy(
                 out=q_grouped[:, qt * I : (qt + 1) * I].rearrange("p (c i t) -> p c t i", i=4, t=PACK),

@@ -21,6 +21,7 @@ PACK = 4
 Q_TILES = Q // P
 HEADS = Q // X
 HALF = I // 2
+BANK = 512
 
 
 def tile_attend_ownlists_gatedkeys_kernel(tc, query, keys, kgate, size, vals, own, offs, out):
@@ -43,9 +44,6 @@ def tile_attend_ownlists_gatedkeys_kernel(tc, query, keys, kgate, size, vals, ow
                 rhs=rhs[0][:, rhs_cols].bitcast(FP8X4), rhs_scale=rhs[1][:, rhs_cols], start=True, stop=True,
             )
 
-        def word(tile, col):
-            return tile[:, col : col + 2].bitcast(F32)
-
         offsets = sb.tile([P, I // 16], U16, name="offsets")
 
         def listed(plane, slots):
@@ -58,7 +56,9 @@ def tile_attend_ownlists_gatedkeys_kernel(tc, query, keys, kgate, size, vals, ow
             nc.sync.dma_start(out=tiles[t][:], in_=src.rearrange("(p t) n -> p t n", t=PACK)[:, t, :])
 
         every, lower, upper = slice(0, I), slice(0, HALF), slice(HALF, I)
+        tile_cols = slice(0, P)
         q_cols = [slice(qt * P, (qt + 1) * P) for qt in range(Q_TILES)]
+        bank = [ps.tile([P, BANK], F32, name="bank" + str(b))[:] for b in range(8)]
 
         gate_pl, key_pl, val_pl = plane_tiles("gate"), plane_tiles("key"), plane_tiles("val")
         size_col = sb.tile([P, PACK], F32, name="size_col")
@@ -80,17 +80,15 @@ def tile_attend_ownlists_gatedkeys_kernel(tc, query, keys, kgate, size, vals, ow
 
         ident = sb.tile([P, P], F32, name="ident")
         make_identity(nc, ident[:])
-
         warm_in = sb.tile([P, 8], F32, name="warm_in")
         nc.gpsimd.memset(warm_in[:], 0.0)
 
-        size_turned = ps.tile([P, PACK, P], F32, name="size_turned")
+        size_turned = bank[0].rearrange("p (t s) -> p t s", t=PACK)
         for t in range(PACK):
             nc.tensor.transpose(size_turned[:, t, :], size_col[:, t : t + 1].to_broadcast([P, P]), ident[:])
 
         km = [sb.tile([P, 2, I], F32, name="km" + str(pair)) for pair in range(2)]
-        km_grouped = sb.tile([P, I * PACK], BF16, name="km_grouped", align_bytes=64)
-        km_rows = km_grouped[:]
+        km_rows = sb.tile([P, I * PACK], BF16, name="km_grouped", align_bytes=64)[:]
         km_view = km_rows.rearrange("p (c i t) -> p c t i", i=4, t=PACK)
         gates = [sb.tile([P, I], F32, name="sig" + str(t)) for t in range(PACK)]
 
@@ -114,28 +112,6 @@ def tile_attend_ownlists_gatedkeys_kernel(tc, query, keys, kgate, size, vals, ow
         weave_keys(1, upper)
 
         q_grouped = sb.tile([P, Q * PACK], BF16, name="q_grouped", align_bytes=64)
-        picked = [sb.tile([P, I], BF16, name="picked" + str(t), align_bytes=64)[:] for t in range(PACK - 1)]
-        w_rows = [sb.tile([P, I], BF16, name="w_rows" + str(qt), align_bytes=64)[:] for qt in range(Q_TILES)]
-        v_grouped = sb.tile([P, PACK * I], BF16, name="v_grouped", align_bytes=64)
-        neg_max = [sb.tile([P, 1], F32, name="neg_max0")[:], v_grouped[:, 0:2].bitcast(F32)]
-
-        def pick(on_scalar, t, slots):
-            if on_scalar:
-                nc.scalar.activation(picked[t][:, slots], listed(val_pl[t], slots), ACT.Copy)
-            else:
-                nc.vector.tensor_copy(picked[t][:, slots], listed(val_pl[t], slots))
-
-        def turn_values(t, bank):
-            words = picked[t].bitcast(F32)
-            for u in range(2):
-                nc.tensor.transpose(bank[:, u, :], words[:, u : I // 2 : 2], ident[:])
-
-        def group(copy, turned, grouped):
-            copy(
-                out=grouped.bitcast(F32).rearrange("p (k m u) -> p k m u", m=P, u=2),
-                in_=turned.rearrange("p k u m -> p k m u"),
-            )
-
         q_mx = mx_tiles(Q, "q")
         km_mx = [mx_tiles(HALF, "km0"), mx_tiles(HALF, "km1", "q_raw", 256)]
         for qt in range(Q_TILES):
@@ -147,23 +123,46 @@ def tile_attend_ownlists_gatedkeys_kernel(tc, query, keys, kgate, size, vals, ow
             quantize(km_mx[half], lower, km_rows[:, half * HALF * PACK : (half + 1) * HALF * PACK])
             quantize(q_mx, q_cols[half], q_grouped[:, half * I : (half + 1) * I])
 
-        scores = [ps.tile([P, I], F32, name="score", tag="score" + str(qt)) for qt in range(Q_TILES)]
+        scores = [bank[1], bank[2]]
         for qt in range(Q_TILES):
             for half, slots in enumerate((lower, upper)):
                 product(scores[qt][:, slots], q_mx, q_cols[qt], km_mx[half], lower)
 
-        pick(True, 0, every)
-        pick(True, 1, every)
-
-        probs = [sb.tile([P, I], F32, name="probs" + str(qt))[:] for qt in range(Q_TILES)]
+        probs = [sb.tile([P, I], F32, name="probs" + str(qt), align_bytes=64)[:] for qt in range(Q_TILES)]
+        middle = HALF * PACK
+        picked = [
+            km_rows[:, middle - HALF : middle + HALF],
+            sb.tile([P, I], BF16, name="picked1", align_bytes=64)[:],
+            sb.tile([P, I], BF16, name="picked2", align_bytes=64)[:],
+            probs[0][:, upper].bitcast(BF16),
+        ]
+        v_grouped = [sb.tile([P, I], BF16, name="v_grouped" + str(t), align_bytes=64)[:] for t in range(PACK)]
+        v_grouped[1] = probs[1][:, upper].bitcast(BF16)
+        w_rows = [sb.tile([P, I], BF16, name="w_rows" + str(qt), align_bytes=64)[:] for qt in range(Q_TILES)]
+        neg_max = [sb.tile([P, 1], F32, name="neg_max0")[:], v_grouped[0][:, 0:2].bitcast(F32)]
         totals = [sb.tile([P, 1], F32, name="total" + str(qt))[:] for qt in range(Q_TILES)]
         inv = [sb.tile([P, 1], F32, name="inv" + str(qt))[:] for qt in range(Q_TILES)]
-        for qt in range(Q_TILES):
-            nc.vector.tensor_reduce(neg_max[qt], scores[qt][:], AXIS.X, ALU.max, negate=True)
-            nc.scalar.activation(
-                probs[qt].rearrange("p (u s e) -> p u s e", u=2, e=2),
-                scores[qt][:].rearrange("p (s u e) -> p u s e", u=2, e=2),
-                ACT.Exp, bias=neg_max[qt], accum_out=totals[qt],
+
+        def pick_scalar(t, slots):
+            nc.scalar.activation(picked[t][:, slots], listed(val_pl[t], slots), ACT.Copy)
+
+        def pick_vector(t, slots):
+            nc.vector.tensor_copy(picked[t][:, slots], listed(val_pl[t], slots))
+
+        def pick_dealt(t):
+            dealt = picked[t].rearrange("p (u s e) -> p s u e", u=2, e=2)
+            nc.scalar.activation(dealt, listed(val_pl[t], every), ACT.Copy)
+
+        def turn(dst, rows, dealt):
+            words = rows.bitcast(F32)
+            for u in range(2):
+                source = words[:, q_cols[u]] if dealt else words[:, u : HALF : 2]
+                nc.tensor.transpose(dst[:, q_cols[u]], source, ident[:])
+
+        def group(copy, turned, grouped):
+            copy(
+                out=grouped.bitcast(F32).rearrange("p (m u) -> p m u", u=2),
+                in_=turned[:, lower].rearrange("p (u m) -> p m u", u=2),
             )
 
         def weigh(qt, u):
@@ -174,67 +173,69 @@ def tile_attend_ownlists_gatedkeys_kernel(tc, query, keys, kgate, size, vals, ow
                 inv[qt], size_turned[:, 2 * u : 2 * u + 2, :].rearrange("p e s -> p s e"), ALU.mult, ALU.mult,
             )
 
-        v01_turned = ps.tile([P, 2, 2, P], F32, name="v01_turned")
-        for t in range(2):
-            turn_values(t, v01_turned[:, t])
-        pick(False, 2, upper)
+        pick_scalar(0, lower)
+        pick_vector(0, upper)
+        pick_scalar(1, every)
+        for qt in range(Q_TILES):
+            nc.vector.tensor_reduce(neg_max[qt], scores[qt], AXIS.X, ALU.max, negate=True)
+            nc.scalar.activation(
+                probs[qt].rearrange("p (u s e) -> p u s e", u=2, e=2),
+                scores[qt].rearrange("p (s u e) -> p u s e", u=2, e=2),
+                ACT.Exp, bias=neg_max[qt], accum_out=totals[qt],
+            )
+
+        v_turned = [bank[1], bank[7], bank[3], bank[2]]
+        w_turned = [bank[3], bank[2]]
+        o_bank = [bank[5], bank[6], bank[4], bank[0]]
+        turn(v_turned[1], picked[1], False)
+        turn(v_turned[0], picked[0], False)
+        pick_vector(2, upper)
         nc.vector.reciprocal(inv[0], totals[0])
         weigh(0, 0)
         nc.vector.reciprocal(inv[1], totals[1])
         weigh(0, 1)
         weigh(1, 0)
         weigh(1, 1)
-        pick(True, 2, lower)
-        w_turned = [ps.tile([P, 1, 2, P], F32, name="w_turned", tag=tag) for tag in ("score0", "score1")]
+        pick_scalar(2, lower)
         for qt in range(Q_TILES):
-            for u in range(2):
-                nc.tensor.transpose(w_turned[qt][:, 0, u, :], w_rows[qt].bitcast(F32)[:, u * P : (u + 1) * P], ident[:])
+            turn(w_turned[qt], w_rows[qt], True)
 
         w_grouped = [sb.tile([P, I], BF16, name="w_grouped" + str(qt), align_bytes=64)[:] for qt in range(Q_TILES)]
         w_mx = mx_tiles(Q, "w")
-        v01_mx = mx_tiles(2 * P, "v01")
-        group(nc.scalar.copy, v01_turned[:], v_grouped[:, 0 : 2 * I])
-        picked.append(probs[0][:, HALF:I].bitcast(BF16))
-        pick(True, 3, every)
-        group(nc.vector.tensor_copy, w_turned[0][:], w_grouped[0])
-        for t, tag in ((2, "score0"), (3, "v3")):
-            turned = ps.tile([P, 1, 2, P], F32, name="v_turned", tag=tag)
-            turn_values(t, turned[:, 0])
-            group(nc.scalar.copy, turned[:], v_grouped[:, t * I : (t + 1) * I])
-
-        quantize(v01_mx, slice(0, 2 * P), v_grouped[:, 0 : 2 * I])
-        group(nc.vector.tensor_copy, w_turned[1][:], w_grouped[1])
+        group(nc.scalar.copy, v_turned[0], v_grouped[0])
+        pick_dealt(3)
+        group(nc.vector.tensor_copy, w_turned[0], w_grouped[0])
+        v_mx = [mx_tiles(P, "v0")]
+        quantize(v_mx[0], tile_cols, v_grouped[0])
+        group(nc.vector.tensor_copy, w_turned[1], w_grouped[1])
+        group(nc.scalar.copy, v_turned[1], v_grouped[1])
+        for t in (2, 3):
+            turn(v_turned[t], picked[t], t == 3)
+            group(nc.scalar.copy, v_turned[t], v_grouped[t])
         for qt in range(Q_TILES):
             quantize(w_mx, q_cols[qt], w_grouped[qt])
+        v_mx.extend([mx_tiles(P, "v1", "w_grouped0"), mx_tiles(P, "v2"), mx_tiles(P, "v3")])
 
         result = sb.tile([P, PACK, X], F32, name="result", align_bytes=64)
         owned = sb.tile([P, 2, Q], F32, name="owned")
         split = sb.tile([P, 2, Q], F32, name="split")
         halves = sb.tile([P, Q], F32, name="halves")
-        early = [ps.tile([P, Q], F32, name="o" + str(t)) for t in range(2)]
-        late = {t: ps.tile([P, Q], F32, name="o" + str(t), tag=tag) for t, tag in ((2, "v01_turned"), (3, "o3"))}
-        late_mx = {2: mx_tiles(P, "v2", "w_grouped0"), 3: mx_tiles(P, "v3")}
 
         def by_halves(ap):
             return ap.rearrange("p (x h i) -> p x h i", h=2, i=4)
 
-        def keep_own_split(t):
-            nc.vector.tensor_tensor(
-                split[:, :, t * P : (t + 1) * P].rearrange("p h (x i) -> p x h i", i=4),
-                by_halves(early[t][:]), by_halves(own_sb[:, t, :]), ALU.mult,
-            )
-
+        for t in range(PACK):
+            if t > 0:
+                quantize(v_mx[t], tile_cols, v_grouped[t])
+            product(o_bank[t][:, 0:Q], v_mx[t], tile_cols, w_mx, slice(0, Q))
         for t in range(2):
-            product(early[t][:], v01_mx, slice(t * P, (t + 1) * P), w_mx, slice(0, Q))
-        quantize(late_mx[2], slice(0, P), v_grouped[:, 2 * I : 3 * I])
-        quantize(late_mx[3], slice(0, P), v_grouped[:, 3 * I : 4 * I])
-        keep_own_split(0)
-        for t in (2, 3):
-            product(late[t][:], late_mx[t], slice(0, P), w_mx, slice(0, Q))
-        keep_own_split(1)
+            nc.vector.tensor_tensor(
+                split[:, :, q_cols[t]].rearrange("p h (x i) -> p x h i", i=4),
+                by_halves(o_bank[t][:, 0:Q]), by_halves(own_sb[:, t, :]), ALU.mult,
+            )
         nc.gpsimd.tensor_tensor(halves[:], split[:, 0, :], split[:, 1, :], ALU.add)
         for t in (2, 3):
-            nc.vector.tensor_tensor(owned[:, t - 2, :], late[t][:], own_sb[:, t, :], ALU.mult)
+            nc.vector.tensor_tensor(owned[:, t - 2, :], o_bank[t][:, 0:Q], own_sb[:, t, :], ALU.mult)
         for t in (2, 3):
             nc.vector.tensor_reduce(
                 result[:, t, :], owned[:, t - 2, :].rearrange("p (x j) -> p x j", j=HEADS), AXIS.X, ALU.add

@@ -52,8 +52,8 @@ def tile_attend_ownlists_gatedkeys_kernel(tc, query, keys, kgate, size, vals, ow
         def plane_tiles(name):
             return [sb.tile([P, T], F32, name=name + str(t), align_bytes=256) for t in range(PACK)]
 
-        def load_plane(tiles, src, t):
-            nc.sync.dma_start(out=tiles[t][:], in_=src.rearrange("(p t) n -> p t n", t=PACK)[:, t, :])
+        def load_plane(tiles, src, t, queue=nc.sync):
+            queue.dma_start(out=tiles[t][:], in_=src.rearrange("(p t) n -> p t n", t=PACK)[:, t, :])
 
         every, lower, upper = slice(0, I), slice(0, HALF), slice(HALF, I)
         tile_cols = slice(0, P)
@@ -66,8 +66,8 @@ def tile_attend_ownlists_gatedkeys_kernel(tc, query, keys, kgate, size, vals, ow
         load_plane(gate_pl, kgate, 0)
         nc.sync.dma_start(offsets[:], offs)
         load_plane(key_pl, keys, 0)
-        load_plane(gate_pl, kgate, 1)
-        load_plane(key_pl, keys, 1)
+        load_plane(gate_pl, kgate, 1, nc.scalar)
+        load_plane(key_pl, keys, 1, nc.scalar)
         for tiles, src in ((gate_pl, kgate), (key_pl, keys)):
             for t in (2, 3):
                 load_plane(tiles, src, t)
@@ -78,10 +78,12 @@ def tile_attend_ownlists_gatedkeys_kernel(tc, query, keys, kgate, size, vals, ow
         own_sb = sb.tile([P, PACK, Q], F32, name="own_sb", align_bytes=256)
         nc.sync.dma_start(out=own_sb[:], in_=own.rearrange("(p t) q -> p t q", t=PACK))
 
-        ident = sb.tile([P, P], F32, name="ident")
-        make_identity(nc, ident[:])
         warm_in = sb.tile([P, 8], F32, name="warm_in")
         nc.gpsimd.memset(warm_in[:], 0.0)
+        warm_gate = sb.tile([P, 8], F32, name="warm_gate")
+        nc.scalar.activation(warm_gate[:], warm_in[:], ACT.Sigmoid)
+        ident = sb.tile([P, P], F32, name="ident")
+        make_identity(nc, ident[:])
 
         size_turned = bank[0].rearrange("p (t s) -> p t s", t=PACK)
         for t in range(PACK):
@@ -129,17 +131,15 @@ def tile_attend_ownlists_gatedkeys_kernel(tc, query, keys, kgate, size, vals, ow
                 product(scores[qt][:, slots], q_mx, q_cols[qt], km_mx[half], lower)
 
         probs = [sb.tile([P, I], F32, name="probs" + str(qt), align_bytes=64)[:] for qt in range(Q_TILES)]
-        middle = HALF * PACK
         picked = [
-            km_rows[:, middle - HALF : middle + HALF],
+            sb.tile([P, I], BF16, name="picked0", align_bytes=64)[:],
             sb.tile([P, I], BF16, name="picked1", align_bytes=64)[:],
             sb.tile([P, I], BF16, name="picked2", align_bytes=64)[:],
             probs[0][:, upper].bitcast(BF16),
         ]
-        v_grouped = [sb.tile([P, I], BF16, name="v_grouped" + str(t), align_bytes=64)[:] for t in range(PACK)]
-        v_grouped[1] = probs[1][:, upper].bitcast(BF16)
+        v_grouped = sb.tile([P, PACK * I], BF16, name="v_grouped", align_bytes=64)[:]
         w_rows = [sb.tile([P, I], BF16, name="w_rows" + str(qt), align_bytes=64)[:] for qt in range(Q_TILES)]
-        neg_max = [sb.tile([P, 1], F32, name="neg_max0")[:], v_grouped[0][:, 0:2].bitcast(F32)]
+        neg_max = [sb.tile([P, 1], F32, name="neg_max0")[:], v_grouped[:, 0:2].bitcast(F32)]
         totals = [sb.tile([P, 1], F32, name="total" + str(qt))[:] for qt in range(Q_TILES)]
         inv = [sb.tile([P, 1], F32, name="inv" + str(qt))[:] for qt in range(Q_TILES)]
 
@@ -161,8 +161,8 @@ def tile_attend_ownlists_gatedkeys_kernel(tc, query, keys, kgate, size, vals, ow
 
         def group(copy, turned, grouped):
             copy(
-                out=grouped.bitcast(F32).rearrange("p (m u) -> p m u", u=2),
-                in_=turned[:, lower].rearrange("p (u m) -> p m u", u=2),
+                out=grouped.bitcast(F32).rearrange("p (k m u) -> p k m u", m=P, u=2),
+                in_=turned.rearrange("p (k u m) -> p k m u", m=P, u=2),
             )
 
         def weigh(qt, u):
@@ -173,8 +173,7 @@ def tile_attend_ownlists_gatedkeys_kernel(tc, query, keys, kgate, size, vals, ow
                 inv[qt], size_turned[:, 2 * u : 2 * u + 2, :].rearrange("p e s -> p s e"), ALU.mult, ALU.mult,
             )
 
-        pick_scalar(0, lower)
-        pick_vector(0, upper)
+        pick_scalar(0, every)
         pick_scalar(1, every)
         for qt in range(Q_TILES):
             nc.vector.tensor_reduce(neg_max[qt], scores[qt], AXIS.X, ALU.max, negate=True)
@@ -184,11 +183,11 @@ def tile_attend_ownlists_gatedkeys_kernel(tc, query, keys, kgate, size, vals, ow
                 ACT.Exp, bias=neg_max[qt], accum_out=totals[qt],
             )
 
-        v_turned = [bank[1], bank[7], bank[3], bank[2]]
-        w_turned = [bank[3], bank[2]]
-        o_bank = [bank[5], bank[6], bank[4], bank[0]]
-        turn(v_turned[1], picked[1], False)
-        turn(v_turned[0], picked[0], False)
+        v_turned = [bank[3][:, lower], bank[3][:, upper], bank[1][:, lower], bank[4][:, lower]]
+        w_turned = [bank[1][:, lower], bank[2][:, lower]]
+        o_bank = [bank[5], bank[6], bank[3], bank[7]]
+        for t in range(2):
+            turn(v_turned[t], picked[t], False)
         pick_vector(2, upper)
         nc.vector.reciprocal(inv[0], totals[0])
         weigh(0, 0)
@@ -202,19 +201,18 @@ def tile_attend_ownlists_gatedkeys_kernel(tc, query, keys, kgate, size, vals, ow
 
         w_grouped = [sb.tile([P, I], BF16, name="w_grouped" + str(qt), align_bytes=64)[:] for qt in range(Q_TILES)]
         w_mx = mx_tiles(Q, "w")
-        group(nc.scalar.copy, v_turned[0], v_grouped[0])
+        v01_mx = mx_tiles(2 * P, "v01")
+        group(nc.scalar.copy, bank[3], v_grouped[:, 0 : 2 * I])
         pick_dealt(3)
         group(nc.vector.tensor_copy, w_turned[0], w_grouped[0])
-        v_mx = [mx_tiles(P, "v0")]
-        quantize(v_mx[0], tile_cols, v_grouped[0])
-        group(nc.vector.tensor_copy, w_turned[1], w_grouped[1])
-        group(nc.scalar.copy, v_turned[1], v_grouped[1])
         for t in (2, 3):
             turn(v_turned[t], picked[t], t == 3)
-            group(nc.scalar.copy, v_turned[t], v_grouped[t])
+            group(nc.scalar.copy, v_turned[t], v_grouped[:, t * I : (t + 1) * I])
+        quantize(v01_mx, lower, v_grouped[:, 0 : 2 * I])
+        group(nc.vector.tensor_copy, w_turned[1], w_grouped[1])
         for qt in range(Q_TILES):
             quantize(w_mx, q_cols[qt], w_grouped[qt])
-        v_mx.extend([mx_tiles(P, "v1", "w_grouped0"), mx_tiles(P, "v2"), mx_tiles(P, "v3")])
+        late_mx = {2: mx_tiles(P, "v2", "w_grouped0"), 3: mx_tiles(P, "v3")}
 
         result = sb.tile([P, PACK, X], F32, name="result", align_bytes=64)
         owned = sb.tile([P, 2, Q], F32, name="owned")
@@ -224,15 +222,20 @@ def tile_attend_ownlists_gatedkeys_kernel(tc, query, keys, kgate, size, vals, ow
         def by_halves(ap):
             return ap.rearrange("p (x h i) -> p x h i", h=2, i=4)
 
-        for t in range(PACK):
-            if t > 0:
-                quantize(v_mx[t], tile_cols, v_grouped[t])
-            product(o_bank[t][:, 0:Q], v_mx[t], tile_cols, w_mx, slice(0, Q))
-        for t in range(2):
+        def keep_own_split(t):
             nc.vector.tensor_tensor(
                 split[:, :, q_cols[t]].rearrange("p h (x i) -> p x h i", i=4),
                 by_halves(o_bank[t][:, 0:Q]), by_halves(own_sb[:, t, :]), ALU.mult,
             )
+
+        for t in range(2):
+            product(o_bank[t][:, 0:Q], v01_mx, q_cols[t], w_mx, slice(0, Q))
+        for t in (2, 3):
+            quantize(late_mx[t], tile_cols, v_grouped[:, t * I : (t + 1) * I])
+        keep_own_split(0)
+        for t in (2, 3):
+            product(o_bank[t][:, 0:Q], late_mx[t], tile_cols, w_mx, slice(0, Q))
+        keep_own_split(1)
         nc.gpsimd.tensor_tensor(halves[:], split[:, 0, :], split[:, 1, :], ALU.add)
         for t in (2, 3):
             nc.vector.tensor_tensor(owned[:, t - 2, :], o_bank[t][:, 0:Q], own_sb[:, t, :], ALU.mult)

from contextlib import ExitStack

import concourse.mybir as mybir
from concourse.masks import make_identity

D, T, I, Q, X, E = 512, 1024, 512, 256, 32, 512
FLOPS = 2 * D * Q * I + 2 * I * E * Q

F32 = mybir.dt.float32
BF16 = mybir.dt.bfloat16
U32 = mybir.dt.uint32
U16 = mybir.dt.uint16
U8 = mybir.dt.uint8
FP8X4 = mybir.dt.float8_e4m3fn_x4
ACT = mybir.ActivationFunctionType
ALU = mybir.AluOpType
AXIS = mybir.AxisListType

P = 128
PACK = 4
Q_TILES = Q // P
HEADS = Q // X
HALF = I // 2
BANK = 512


def tile_attend_ownlists_gatedkeys_kernel(tc, query, keys, kgate, size, vals, own, offs, out):
    nc = tc.nc
    with ExitStack() as ctx:
        sb = ctx.enter_context(tc.tile_pool(name="sb", bufs=1))
        ps = ctx.enter_context(tc.psum_pool(name="ps", bufs=1))

        def mx_tiles(width, name, tag="", align=64):
            codes = sb.tile([P, width], U32, name=name + "_codes", tag=tag or name + "_codes", align_bytes=align)
            scales = sb.tile([P, width], U8, name=name + "_scales", align_bytes=64)
            return codes, scales

        def quantize(mx, cols, grouped):
            nc.vector.quantize_mx(out=mx[0][:, cols].bitcast(FP8X4), scales=mx[1][:, cols], in_=grouped)

        def product(dst, lhs, lhs_cols, rhs, rhs_cols):
            nc.tensor.matmul_mx(
                out=dst, lhsT=lhs[0][:, lhs_cols].bitcast(FP8X4), lhsT_scale=lhs[1][:, lhs_cols],
                rhs=rhs[0][:, rhs_cols].bitcast(FP8X4), rhs_scale=rhs[1][:, rhs_cols], start=True, stop=True,
            )

        offsets = sb.tile([P, I // 16], U16, name="offsets")

        def listed(plane, slots):
            return plane[:].indirect(offsets[:, slots.start // 16 : slots.stop // 16])

        def plane_tiles(name):
            return [sb.tile([P, T], F32, name=name + str(t), align_bytes=256) for t in range(PACK)]

        def load_plane(tiles, src, t, queue=nc.sync):
            queue.dma_start(out=tiles[t][:], in_=src.rearrange("(p t) n -> p t n", t=PACK)[:, t, :])

        every, lower, upper = slice(0, I), slice(0, HALF), slice(HALF, I)
        tile_cols = slice(0, P)
        q_cols = [slice(qt * P, (qt + 1) * P) for qt in range(Q_TILES)]
        bank = [ps.tile([P, BANK], F32, name="bank" + str(b))[:] for b in range(8)]

        gate_pl, key_pl, val_pl = plane_tiles("gate"), plane_tiles("key"), plane_tiles("val")
        size_col = sb.tile([P, PACK], F32, name="size_col")
        nc.scalar.dma_start(out=size_col[:], in_=size.rearrange("o (p t) -> (o p) t", t=PACK))
        load_plane(gate_pl, kgate, 0)
        nc.sync.dma_start(offsets[:], offs)
        load_plane(key_pl, keys, 0)
        load_plane(gate_pl, kgate, 1, nc.scalar)
        load_plane(key_pl, keys, 1, nc.scalar)
        for tiles, src in ((gate_pl, kgate), (key_pl, keys)):
            for t in (2, 3):
                load_plane(tiles, src, t)
        q_raw = sb.tile([P, PACK, Q], F32, name="q_raw", align_bytes=256)
        nc.sync.dma_start(out=q_raw[:], in_=query.rearrange("(p t) q -> p t q", t=PACK))
        for t in range(PACK):
            load_plane(val_pl, vals, t)
        own_sb = sb.tile([P, PACK, Q], F32, name="own_sb", align_bytes=256)
        nc.sync.dma_start(out=own_sb[:], in_=own.rearrange("(p t) q -> p t q", t=PACK))

        warm_in = sb.tile([P, 8], F32, name="warm_in")
        nc.gpsimd.memset(warm_in[:], 0.0)
        warm_gate = sb.tile([P, 8], F32, name="warm_gate")
        nc.scalar.activation(warm_gate[:], warm_in[:], ACT.Sigmoid)
        ident = sb.tile([P, P], F32, name="ident")
        make_identity(nc, ident[:])

        size_turned = bank[0].rearrange("p (t s) -> p t s", t=PACK)
        for t in range(PACK):
            nc.tensor.transpose(size_turned[:, t, :], size_col[:, t : t + 1].to_broadcast([P, P]), ident[:])

        km = [sb.tile([P, 2, I], F32, name="km" + str(pair)) for pair in range(2)]
        km_rows = sb.tile([P, I * PACK], BF16, name="km_grouped", align_bytes=64)[:]
        km_view = km_rows.rearrange("p (c i t) -> p c t i", i=4, t=PACK)
        gates = [sb.tile([P, I], F32, name="sig" + str(t)) for t in range(PACK)]

        def weave_keys(pair, slots):
            nc.vector.tensor_copy(
                out=km_view[:, slots.start // 4 : slots.stop // 4, 2 * pair : 2 * pair + 2, :],
                in_=km[pair][:, :, slots].rearrange("p t (c i) -> p c t i", i=4),
            )

        for t in range(PACK):
            nc.scalar.activation(gates[t][:], listed(gate_pl[t], every), ACT.Sigmoid)
            for slots in (every,) if t < PACK - 1 else (lower, upper):
                nc.vector.tensor_tensor(
                    km[t // 2][:, t % 2, slots], listed(key_pl[t], slots), gates[t][:, slots], ALU.mult
                )
            if t == 1:
                weave_keys(0, every)
        warm_out = sb.tile([P, 8], F32, name="warm_out", tag="gate3", align_bytes=256)
        nc.scalar.activation(warm_out[:], warm_in[:], ACT.Exp)
        weave_keys(1, lower)
        weave_keys(1, upper)

        q_grouped = sb.tile([P, Q * PACK], BF16, name="q_grouped", align_bytes=64)
        q_mx = mx_tiles(Q, "q")
        km_mx = [mx_tiles(HALF, "km0"), mx_tiles(HALF, "km1", "q_raw", 256)]
        for qt in range(Q_TILES):
            nc.scalar.copy(
                out=q_grouped[:, qt * I : (qt + 1) * I].rearrange("p (c i t) -> p c t i", i=4, t=PACK),
                in_=q_raw[:, :, q_cols[qt]].rearrange("p t (c i) -> p c t i", i=4),
            )
        for half in range(2):
            quantize(km_mx[half], lower, km_rows[:, half * HALF * PACK : (half + 1) * HALF * PACK])
            quantize(q_mx, q_cols[half], q_grouped[:, half * I : (half + 1) * I])

        scores = [bank[1], bank[2]]
        for qt in range(Q_TILES):
            for half, slots in enumerate((lower, upper)):
                product(scores[qt][:, slots], q_mx, q_cols[qt], km_mx[half], lower)

        probs = [sb.tile([P, I], F32, name="probs" + str(qt), align_bytes=64)[:] for qt in range(Q_TILES)]
        picked = [
            sb.tile([P, I], BF16, name="picked0", align_bytes=64)[:],
            sb.tile([P, I], BF16, name="picked1", align_bytes=64)[:],
            sb.tile([P, I], BF16, name="picked2", align_bytes=64)[:],
            probs[0][:, upper].bitcast(BF16),
        ]
        v_grouped = sb.tile([P, PACK * I], BF16, name="v_grouped", align_bytes=64)[:]
        w_rows = [sb.tile([P, I], BF16, name="w_rows" + str(qt), align_bytes=64)[:] for qt in range(Q_TILES)]
        neg_max = [sb.tile([P, 1], F32, name="neg_max0")[:], v_grouped[:, 0:2].bitcast(F32)]
        totals = [sb.tile([P, 1], F32, name="total" + str(qt))[:] for qt in range(Q_TILES)]
        inv = [sb.tile([P, 1], F32, name="inv" + str(qt))[:] for qt in range(Q_TILES)]

        def pick_scalar(t, slots):
            nc.scalar.activation(picked[t][:, slots], listed(val_pl[t], slots), ACT.Copy)

        def pick_vector(t, slots):
            nc.vector.tensor_copy(picked[t][:, slots], listed(val_pl[t], slots))

        def pick_dealt(t):
            dealt = picked[t].rearrange("p (u s e) -> p s u e", u=2, e=2)
            nc.scalar.activation(dealt, listed(val_pl[t], every), ACT.Copy)

        def turn(dst, rows, dealt):
            words = rows.bitcast(F32)
            for u in range(2):
                source = words[:, q_cols[u]] if dealt else words[:, u : HALF : 2]
                nc.tensor.transpose(dst[:, q_cols[u]], source, ident[:])

        def group(copy, turned, grouped):
            copy(
                out=grouped.bitcast(F32).rearrange("p (k m u) -> p k m u", m=P, u=2),
                in_=turned.rearrange("p (k u m) -> p k m u", m=P, u=2),
            )

        def weigh(qt, u):
            places = slice(u * HALF, (u + 1) * HALF)
            nc.vector.scalar_tensor_tensor(
                w_rows[qt][:, places].rearrange("p (s e) -> p s e", e=2),
                probs[qt][:, places].rearrange("p (s e) -> p s e", e=2),
                inv[qt], size_turned[:, 2 * u : 2 * u + 2, :].rearrange("p e s -> p s e"), ALU.mult, ALU.mult,
            )

        pick_scalar(0, every)
        pick_scalar(1, every)
        for qt in range(Q_TILES):
            nc.vector.tensor_reduce(neg_max[qt], scores[qt], AXIS.X, ALU.max, negate=True)
            nc.scalar.activation(
                probs[qt].rearrange("p (u s e) -> p u s e", u=2, e=2),
                scores[qt].rearrange("p (s u e) -> p u s e", u=2, e=2),
                ACT.Exp, bias=neg_max[qt], accum_out=totals[qt],
            )

        v_turned = [bank[3][:, lower], bank[3][:, upper], bank[1][:, lower], bank[4][:, lower]]
        w_turned = [bank[1][:, lower], bank[2][:, lower]]
        o_bank = [bank[5], bank[6], bank[3], bank[7]]
        for t in range(2):
            turn(v_turned[t], picked[t], False)
        pick_vector(2, upper)
        nc.vector.reciprocal(inv[0], totals[0])
        weigh(0, 0)
        nc.vector.reciprocal(inv[1], totals[1])
        weigh(0, 1)
        weigh(1, 0)
        weigh(1, 1)
        pick_scalar(2, lower)
        for qt in range(Q_TILES):
            turn(w_turned[qt], w_rows[qt], True)

        w_grouped = [sb.tile([P, I], BF16, name="w_grouped" + str(qt), align_bytes=64)[:] for qt in range(Q_TILES)]
        w_mx = mx_tiles(Q, "w")
        v01_mx = mx_tiles(2 * P, "v01")
        group(nc.scalar.copy, bank[3], v_grouped[:, 0 : 2 * I])
        pick_dealt(3)
        group(nc.vector.tensor_copy, w_turned[0], w_grouped[0])
        for t in (2, 3):
            turn(v_turned[t], picked[t], t == 3)
            group(nc.scalar.copy, v_turned[t], v_grouped[:, t * I : (t + 1) * I])
        quantize(v01_mx, lower, v_grouped[:, 0 : 2 * I])
        group(nc.vector.tensor_copy, w_turned[1], w_grouped[1])
        for qt in range(Q_TILES):
            quantize(w_mx, q_cols[qt], w_grouped[qt])
        late_mx = {2: mx_tiles(P, "v2", "w_grouped0"), 3: mx_tiles(P, "v3")}

        result = sb.tile([P, PACK, X], F32, name="result", align_bytes=64)
        owned = sb.tile([P, 2, Q], F32, name="owned")
        split = sb.tile([P, 2, Q], F32, name="split")
        halves = sb.tile([P, Q], F32, name="halves")

        def by_halves(ap):
            return ap.rearrange("p (x h i) -> p x h i", h=2, i=4)

        def keep_own_split(t):
            nc.vector.tensor_tensor(
                split[:, :, q_cols[t]].rearrange("p h (x i) -> p x h i", i=4),
                by_halves(o_bank[t][:, 0:Q]), by_halves(own_sb[:, t, :]), ALU.mult,
            )

        for t in range(2):
            product(o_bank[t][:, 0:Q], v01_mx, q_cols[t], w_mx, slice(0, Q))
        for t in (2, 3):
            quantize(late_mx[t], tile_cols, v_grouped[:, t * I : (t + 1) * I])
        keep_own_split(0)
        for t in (2, 3):
            product(o_bank[t][:, 0:Q], late_mx[t], tile_cols, w_mx, slice(0, Q))
        keep_own_split(1)
        nc.gpsimd.tensor_tensor(halves[:], split[:, 0, :], split[:, 1, :], ALU.add)
        for t in (2, 3):
            nc.vector.tensor_tensor(owned[:, t - 2, :], o_bank[t][:, 0:Q], own_sb[:, t, :], ALU.mult)
        for t in (2, 3):
            nc.vector.tensor_reduce(
                result[:, t, :], owned[:, t - 2, :].rearrange("p (x j) -> p x j", j=HEADS), AXIS.X, ALU.add
            )
        out_planes = out.rearrange("(p t) x -> p t x", t=PACK)
        nc.scalar.dma_start(out=out_planes[:, 2:4, :], in_=result[:, 2:4, :])
        nc.vector.tensor_reduce(
            result[:, 0:2, :], halves[:].rearrange("p (t x i) -> p t x i", t=2, i=4), AXIS.X, ALU.add
        )
        nc.sync.dma_start(out=out_planes[:, 0:2, :], in_=result[:, 0:2, :])
